import numpy as np, ml_dtypes
CORES = [36,164,52,180,100,228,116,244]
N = 8
import mx_ref
BF = ml_dtypes.bfloat16
def entries(a):
    return np.ascontiguousarray(a.T).reshape(-1)
def table(e):
    return np.ascontiguousarray(np.reshape(e, (-1, 16)).T).astype(np.int32)
def pick(q, e):
    c = np.concatenate([q[0].reshape(128, -1, 4), np.zeros((128, 1, 4), np.uint8)], axis=1); s = np.concatenate([q[1], np.ones((16, 1), np.uint8)], axis=1)
    return (np.ascontiguousarray(c[:, e].reshape(128, -1)), np.ascontiguousarray(s[:, e]))
def join(*qs):
    return (np.concatenate([q[0] for q in qs], axis=1), np.concatenate([q[1] for q in qs], axis=1))
def put(q, e, v):
    c, s = q[0].reshape(128, -1, 4).copy(), q[1].copy(); c[:, e] = v[0].reshape(128, -1, 4); s[:, e] = v[1]
    return (c.reshape(128, -1), s)
def pk(c, s):
    return (np.ascontiguousarray(c), mx_ref.live(s))
def emit(q):
    return q[0], q[1]
def packed(v, rng):
    q = [mx_ref.quantize(np.ascontiguousarray(v[r])) for r in range(N)]
    return np.stack([a for a, b in q]), np.stack([mx_ref.plane(b, rng) for a, b in q])
def decode(q):
    o = []
    for b in range(4):
        e = np.zeros((128, 128, 4), np.float32); e[np.arange(128), np.arange(128), b] = 1
        o.append(mx_ref.matmul(mx_ref.quantize(e.reshape(128, 512).astype(BF)), q))
    return np.stack(o, axis=2).reshape(128, -1)
def f(rng, *shape):
    return mx_ref.flush((rng.standard_normal(shape, dtype=np.float32) * np.exp2(rng.integers(-2, 3, shape[:-1] + (1,)))).astype(BF))
def wide(rng, *shape, cols=0):
    v = rng.standard_normal(shape, dtype=np.float32) * np.exp2(rng.integers(-12, 13, shape)).astype(np.float32)
    if cols: v *= np.repeat(np.exp2(rng.integers(-cols, cols + 1, shape[:-2] + (1, shape[-1] // 4))) * (rng.random(shape[:-2] + (1, shape[-1] // 4)) > 0.0625), 4, axis=-1).astype(np.float32)
    return mx_ref.flush(v.astype(BF))
C, S, CAPP = 512, 256, 48
def big(v, k):
    v = v.astype(np.float32) * np.float32(k)
    v[np.abs(v) < np.float32(2.0 ** -16)] = 0
    return v.astype(BF)
def names(rng, n, each):
    out, at, m = [None] * N, 0, int(n.sum())
    if not each:
        left = np.full(C, 2)
        for s in rng.permutation(N):
            out[s] = rng.permutation(np.flatnonzero(left))[:n[s]]; left[out[s]] -= 1
        return out
    a = rng.permutation(C)[:m // each]
    if each == 2: a = np.concatenate([a, rng.permutation(a)])
    for s in rng.permutation(N):
        out[s] = a[at:at + n[s]]; at += n[s]
    return out
def lists(rng, each=0, full=False, gaps=False, silent=False):
    sn, tc = np.full((N, N * CAPP), -1), np.full((N, N * CAPP), -1)
    n = np.full((N, N), CAPP) if full else rng.integers(CAPP // 4, CAPP, (N, N))
    if gaps: n[:] = CAPP - CAPP // 6
    if silent: n[:, int(rng.integers(0, N))] = 0
    for q in range(N):
        t = names(rng, n[:, q], each)
        for s in range(N): tc[q, s * CAPP + rng.permutation(CAPP)[:n[s, q]]] = t[s]
    for s in range(N):
        used = np.concatenate([tc[q, s * CAPP:s * CAPP + CAPP] >= 0 for q in range(N)])
        e = np.concatenate([rng.permutation(S), rng.integers(0, S, N * CAPP)])[:used.sum()]
        sn[s, used] = rng.permutation(e)
    return {"sn": np.stack([table(v) for v in sn]), "tc": np.stack([table(v) for v in tc])}
def setup_inputs(rng):
    c, p = packed(big(f(rng, N, 128, 4 * C), 1), rng)
    return {"wc": c, "ws": p, "gr": big(f(rng, N, 128, 4 * S), 8), **lists(rng)}
def setup_inputs_cancel(rng):
    tc, P = lists(rng, each=2, full=True, gaps=True)["tc"], S // 2
    x = rng.integers(4, 8, (128, P, 4)) * np.exp2(rng.integers(-2, 1, (128, P, 4))) * rng.choice([-1.0, 1.0], (128, P, 4)) * np.exp2(rng.integers(-2, 3, (128, P, 1)))
    h = rng.integers(0, P, (N, C))
    c, p = packed(np.stack([x[:, h[q]].reshape(128, -1) for q in range(N)]).astype(np.float32).astype(BF), rng)
    g, sn = np.zeros((N, 128, S, 4), np.float32), np.full((N, N * CAPP), -1)
    at = np.stack([rng.permutation(S) for s in range(N)])
    for s in range(N):
        g[s][:, at[s, :P]] = 8 * x
        g[s][:, at[s, P:]] = 8 * x * np.exp2(-rng.integers(21, 25, (P, 1)))
    for q in range(N):
        t = entries(tc[q]).reshape(N, CAPP)
        o = rng.permutation(np.unique(t[t >= 0]))
        late, seen = np.zeros(C, bool), np.zeros(C, bool)
        late[o[:o.size // 2]] = True
        for s in range(N):
            k = np.flatnonzero(t[s] >= 0); e = t[s][k]
            small = seen[e] != late[e]
            sn[s, q * CAPP + k] = at[s][P * small + h[q, e]]
            seen[e] = True
    return {"wc": c, "ws": p, "gr": g.reshape(N, 128, 4 * S).astype(BF), "sn": np.stack([table(v) for v in sn]), "tc": tc}
def setup_inputs_full(rng):
    return {**setup_inputs(rng), **lists(rng, full=True)}
def setup_inputs_most(rng):
    return {**setup_inputs(rng), **lists(rng, each=1, full=True, silent=True)}
def setup_inputs_spread(rng):
    d = setup_inputs(rng)
    d["wc"], d["ws"] = packed(big(wide(rng, N, 128, 4 * C, cols=8), 1), rng)
    d["gr"] = big(wide(rng, N, 128, 4 * S, cols=8), 8)
    return d
def setup_inputs_twice(rng):
    return {**setup_inputs(rng), **lists(rng, each=2, full=True)}
def check_inputs(d):
    b = []
    for r in range(N):
        a, t = entries(d["sn"][r]), entries(d["tc"][r])
        if a.min() < -1 or a.max() >= S: b.append("sn")
        sent = np.concatenate([entries(d["sn"][s])[r * CAPP:r * CAPP + CAPP] for s in range(N)])
        bad = t.min() < -1 or t.max() >= C or ((t >= 0) != (sent >= 0)).any()
        for s in range(N):
            v = t[s * CAPP:s * CAPP + CAPP]; v = v[v >= 0]
            bad = bad or len(set(v.tolist())) != v.size
        if bad or (np.unique(t[t >= 0], return_counts=True)[1] > 2).any(): b.append("tc")
    return b
def reference(wc, ws, gr, sn, tc):
    oc, osc, up = np.zeros((N, 128, 4 * C), np.uint8), np.zeros((N, 16, C), np.uint8), np.zeros((N, 1, C), np.float32)
    g = [decode(mx_ref.quantize(np.ascontiguousarray(gr[s]))).reshape(128, S, 4) for s in range(N)]
    for q in range(N):
        w = pk(wc[q], ws[q])
        v = decode(w).reshape(128, C, 4)
        for s in range(N):
            e, t = entries(sn[s])[q * CAPP:q * CAPP + CAPP], entries(tc[q])[s * CAPP:s * CAPP + CAPP]
            k = t >= 0
            v[:, t[k]] = v[:, t[k]] - g[s][:, e[k]] * np.float32(0.125)
            up[q, 0, t[k]] += 1
        named = np.flatnonzero(up[q, 0])
        new = mx_ref.quantize(np.ascontiguousarray(v.reshape(128, -1).astype(BF)))
        oc[q], osc[q] = emit(put(w, named, pick(new, named)))
    return {"oc": oc, "osc": osc, "up": up}

@@ -1,0 +1,269 @@
+from concourse.bass import DstId, RemoteDMATransfer
+from concourse.mybir import dt, AluOpType as op, ActivationFunctionType
+
+X4, U8 = "float8_e4m3fn_x4", "uint8"
+C, S, CAPP, N = 512, 256, 48, 8
+NS = N * CAPP
+HALF = NS // 2
+ZC = 128
+NP = NS - CAPP
+NV = 352
+FW = C + 160
+MID, NONE = 192, 768
+LC = NS // 16
+BF_, BV = C // 32, NV // 32
+NB = BF_ + BV
+
+SCRATCH = {
+    "grt": ("sbuf", [128, 4 * S], "bfloat16"),
+    "sni": ("sbuf", [128, LC], "int32"), "tci": ("sbuf", [128, 28], "int32"),
+    "soff": ("sbuf", [128, LC], "uint16"), "woff": ("sbuf", [128, LC], "uint16"),
+    "gq": ("sbuf", [128, S], X4), "gqs": ("sbuf", [128, S], U8),
+    "gp": ("sbuf", [128, NS], X4), "gps": ("sbuf", [128, NS], U8),
+    "land": ("sbuf", [128, NS + ZC], X4), "lands": ("sbuf", [128, NS + ZC], U8),
+    "w2": ("sbuf", [128, C], X4), "w2s": ("sbuf", [128, C], U8),
+    "wsl": ("sbuf", [128, NS], X4), "wsls": ("sbuf", [128, NS], U8),
+    "pk": ("sbuf", [128, NS], X4), "pks": ("sbuf", [128, NS], U8),
+    "wn": ("sbuf", [128, NS + C], X4), "wns": ("sbuf", [128, NS + C], U8),
+    "on": ("sbuf", [128, C], X4), "ons": ("sbuf", [128, C], U8),
+    "zer": ("sbuf", [128, 516], "bfloat16"), "eb": ("sbuf", [128, 516], "bfloat16"), "e2": ("sbuf", [128, 516], "bfloat16"),
+    "q1": ("sbuf", [128, 512], X4), "q1s": ("sbuf", [128, 512], U8),
+    "q2": ("sbuf", [128, 512], X4), "q2s": ("sbuf", [128, 512], U8),
+    "k1": ("sbuf", [128, 28], "int32"), "t2": ("sbuf", [128, 28], "int32"), "t3": ("sbuf", [128, 28], "int32"),
+    "toff": ("sbuf", [128, 28], "uint16"),
+    "vals": ("sbuf", [128, CAPP], "bfloat16"),
+    "fb": ("sbuf", [128, FW], "bfloat16"),
+    "vv": ("sbuf", [128, NV], "bfloat16"),
+    "tt": ("sbuf", [128, C + NV], "bfloat16"),
+    "sa": ("sbuf", [128, 32], "float32"), "sb": ("sbuf", [128, 32], "float32"), "sc": ("sbuf", [128, 32], "float32"),
+    "ma": ("sbuf", [128, 16], "float32"), "mb": ("sbuf", [128, 16], "float32"), "mc": ("sbuf", [128, 16], "float32"),
+    "kf": ("sbuf", [128, 16], "float32"), "kv": ("sbuf", [128, 16], "float32"), "dv": ("sbuf", [128, 16], "float32"),
+    "r": ("sbuf", [128, 32], "float32"), "z": ("sbuf", [128, 64], "float32"), "y": ("sbuf", [128, 64], "float32"),
+    "lst": ("sbuf", [128, 64], "uint16"),
+    "u0": ("sbuf", [128, 16], "float32"), "u1": ("sbuf", [128, 16], "float32"),
+    "ub": ("sbuf", [128, 32], "float32"), "ut": ("sbuf", [128, 32], "float32"),
+    "h": ("sbuf", [128, 4 * NS], "bfloat16"),
+    "psa": ("psum", [128, 2048], "float32"), "psb": ("psum", [128, 2048], "float32"),
+}
+SEMAPHORES = ["ldg", "lds", "ldt", "ldw", "ldn", "ownc", "owns", "st", "arc", "ars", "sent", "v", "z", "gi", "ea", "e2r", "eq1", "eq2", "soffr", "gqr", "gpc", "gpp",
+              "woffr", "tof", "fg", "vg", "wpc", "wps", "listr", "utr", "ons0", "ons1", "onc0", "onc1"] + \
+             [k + h for k in ("pc", "pp", "hs", "qn") for h in "ab"] + ["t%s%d" % (h, b) for h in "ab" for b in range(4)]
+
+
+def rank_program(g, core, T, topo):
+    rank = T.rank_of(core)
+    if rank is None:
+        return
+    V, P, A, Y = g.vector, g.tensor, g.scalar, g.sync
+    COPY = ActivationFunctionType.Copy
+    total, seen, mine = {}, {}, {}
+
+    def inc(ins, name, n=1):
+        ins.then_inc(T.sem[name], n)
+        total[name] = total.get(name, 0) + n
+        return name
+
+    def wait(qn, q, *evs):
+        for name in evs:
+            if seen.get((qn, name), 0) < total[name]:
+                q.wait_ge(T.sem[name], total[name])
+                seen[(qn, name)] = total[name]
+
+    def vi(ins, name="v"):
+        mine[inc(ins, name)] = 1
+
+    def vdep():
+        wait("v", V, *sorted(mine))
+        mine.clear()
+
+    def u8(v):
+        return v.bitcast(dt.uint8)
+
+    def u32(v):
+        return v.bitcast(dt.uint32)
+
+    inc(Y.dma_start(T.grt[:, 0:2 * S], T.gr[:, 0:2 * S]), "ldg", 16)
+    inc(A.dma_start(T.grt[:, 2 * S:4 * S], T.gr[:, 2 * S:4 * S]), "ldg", 16)
+    for k in range(N):
+        inc((Y, A)[k % 2].dma_start(T.sni[16 * k:16 * k + 16, :], T.sn[:]), "lds", 16)
+    for k in range(N):
+        inc((Y, A)[k % 2].dma_start(T.tci[16 * k:16 * k + 16, 0:LC], T.tc[:]), "ldt", 16)
+    for k in range(N):
+        inc(Y.dma_start(T.tci[16 * k:16 * k + 16, LC:LC + 3], T.tc[:, 3 * k:3 * k + 3]), "ldt", 16)
+    inc(Y.dma_start(u8(T.w2[:]), T.wc[:]), "ldw", 16)
+    inc(A.dma_start(T.w2s[:], T.ws[:]), "ldw", 16)
+
+    F32 = {"allow_small_or_imprecise_dtypes": True}
+    vi(V.memset(T.zer[:], 0.0), "z")
+    inc(g.iota(T.k1[:, 0:LC + 3], [[0, N + 1], [16, 3]], C, 1), "gi")
+    wait("g", g, "z")
+    inc(g.affine_select(T.eb[:], T.zer[:], [[1, 516]], op.not_equal, 1.0, -3, -4), "ea")
+    inc(g.iota(T.vals[:], [[1, CAPP]], -MID, 3, **F32), "gi")
+    inc(g.iota(T.kf[0:32, :], [[32, BF_]], NS - MID, 1, **F32), "gi")
+    inc(g.iota(T.kv[0:32, 0:BV], [[32, BV]], 6 * NONE - MID, 1, **F32), "gi")
+    vi(V.memset(T.fb[:], float(NONE)))
+    vi(V.memset(T.r[:], 0.0))
+    vi(V.memset(T.ub[:], 0.0))
+    vdep()
+    vi(V.quantize_mx(T.land[:, NS:NS + ZC], T.lands[:, NS:NS + ZC], T.zer[:, 0:4 * ZC]))
+    wait("a", A, "ea")
+    inc(A.activation(T.e2[:], T.eb[:], COPY, scale=-0.125), "e2r")
+    wait("v", V, "ea")
+    for b in range(4):
+        vi(V.quantize_mx(T.q1[:, 128 * b:128 * b + 128], T.q1s[:, 128 * b:128 * b + 128], T.eb[:, 3 - b:515 - b]), "eq1")
+
+    wait("v", V, "lds")
+    vi(V.tensor_copy(T.soff[:], T.sni[:]), "soffr")
+    wait("v", V, "ldg")
+    vi(V.quantize_mx(T.gq[:], T.gqs[:], T.grt[:]), "gqr")
+    vdep()
+    vi(V.tensor_copy(u32(T.gp[:, 0:NS]), u32(T.gq[:, 0:S]).indirect(T.soff[:])), "gpc")
+    wait("a", A, "soffr", "gqr")
+    inc(A.activation(T.gps[:, 0:NS], T.gqs[:, 0:S].indirect(T.soff[:]), COPY), "gpp")
+
+    dests = [(rank + k) % N for k in range(1, N)]
+    lo = CAPP * rank
+
+    def transfers(scales):
+        out = []
+        for k, q in enumerate(dests):
+            d = T.cores[q]
+            rid, pid = topo.addr(d, core)
+            a = CAPP * q
+            src = T.gps[:, a:a + CAPP] if scales else u8(T.gp[:, a:a + CAPP])
+            dst = T.lands[:, lo:lo + CAPP] if scales else u8(T.land[:, lo:lo + CAPP])
+            out.append(RemoteDMATransfer(dst_ids=[DstId(rid=rid, pnc=pid)], dma_engine_mask=1 << topo.engines(core, d)[k],
+                                         remote_sem=T.sem.ars if scales else T.sem.arc, src=src, dst=dst))
+        return out
+
+    wait("g", g, "gpc")
+    g.remote_dma_fused(transfers(False), local_sem=T.sem.sent)
+    wait("g", g, "gpp")
+    g.remote_dma_fused(transfers(True), local_sem=T.sem.sent)
+    total["sent"] = 2 * len(dests)
+    total["arc"] = total["ars"] = len(dests)
+    wait("y", Y, "gpc")
+    inc(Y.dma_start(u8(T.land[:, lo:lo + CAPP]), u8(T.gp[:, lo:lo + CAPP])), "ownc", 16)
+    wait("y", Y, "gpp")
+    inc(Y.dma_start(T.lands[:, lo:lo + CAPP], T.gps[:, lo:lo + CAPP]), "owns", 16)
+    wait("y", Y, "sent")
+    inc(Y.dma_start(u8(T.wn[:, NS:NS + C]), T.wc[:]), "ldn", 16)
+    inc(Y.dma_start(T.wns[:, NS:NS + C], T.ws[:]), "ldn", 16)
+
+    wait("v", V, "ldt", "gi")
+    vi(V.tensor_scalar(T.t2[:, 0:LC + 3], T.tci[:, 0:LC + 3], 1023, None, op.bitwise_and))
+    vi(V.tensor_copy(T.woff[:], T.tci[:, 0:LC]), "woffr")
+    vdep()
+    vi(V.tensor_tensor(T.t3[:, 0:LC + 3], T.t2[:, 0:LC + 3], T.k1[:, 0:LC + 3], op.min))
+    vdep()
+    vi(V.tensor_copy(T.toff[:, 0:LC + 3], T.t3[:, 0:LC + 3]), "tof")
+    vdep()
+    vi(V.tensor_copy(T.fb[:, 0:FW].indirect(T.toff[:, LC:LC + 3]), T.vals[:]), "fg")
+    wait("a", A, "fg", "tof")
+    inc(A.activation(T.vv[:], T.fb[:, 0:FW].indirect(T.toff[:, 0:NV // 16]), COPY), "vg")
+    wait("a", A, "woffr", "ldw")
+    inc(A.activation(T.wsls[:], T.w2s[:, 0:C].indirect(T.woff[:]), COPY), "wps")
+    wait("v", V, "e2r")
+    for b in range(4):
+        vi(V.quantize_mx(T.q2[:, 128 * b:128 * b + 128], T.q2s[:, 128 * b:128 * b + 128], T.e2[:, 3 - b:515 - b]), "eq2")
+    wait("v", V, "ldw")
+    vi(V.tensor_copy(u32(T.wsl[:]), u32(T.w2[:, 0:C]).indirect(T.woff[:])), "wpc")
+    wait("v", V, "fg")
+    vi(V.transpose(T.tt[:, 0:C], T.fb[:, 0:C]))
+    wait("v", V, "vg")
+    vi(V.transpose(T.tt[:, C:C + NV], T.vv[:]))
+    vdep()
+    vi(V.tensor_tensor(T.ma[:], T.tt[:, 0:C:32], T.tt[:, 16:C:32], op.min))
+    vi(V.tensor_tensor(T.sa[:, 0:NB], T.tt[:, 0:C + NV:32], T.tt[:, 16:C + NV:32], op.add))
+    vdep()
+    vi(V.tensor_tensor(T.mb[0:64, :], T.ma[0:64, :], T.ma[64:128, :], op.min))
+    vdep()
+    vi(V.tensor_tensor(T.sb[0:64, 0:NB], T.sa[0:64, 0:NB], T.sa[64:128, 0:NB], op.add))
+    vdep()
+    vi(V.tensor_tensor(T.mc[0:32, :], T.mb[0:32, :], T.mb[32:64, :], op.min))
+    vdep()
+    vi(V.tensor_tensor(T.sc[0:32, 0:NB], T.sb[0:32, 0:NB], T.sb[32:64, 0:NB], op.add))
+    vdep()
+    vi(V.tensor_tensor(T.dv[0:32, 0:BV], T.sc[0:32, BF_:NB], T.kv[0:32, 0:BV], op.subtract))
+    vi(V.tensor_tensor(T.r[0:32, 0:BF_], T.mc[0:32, :], T.kf[0:32, :], op.min))
+    vdep()
+    vi(V.tensor_scalar(T.r[0:32, BF_:NB], T.dv[0:32, 0:BV], float(NS - MID), None, op.min))
+    vdep()
+    vi(V.transpose(T.z[0:32, 16:48], T.r[0:32, :]))
+    vdep()
+    vi(V.tensor_copy(T.z[0:32, 0:16], T.z[0:32, 16:32]))
+    vi(V.tensor_copy(T.z[0:32, 48:64], T.z[0:32, 32:48]))
+    vdep()
+    vi(V.transpose(T.y[0:32, :], T.z[0:32, :]))
+    vdep()
+    for k in range(2):
+        vi(V.tensor_scalar(T.lst[0:32, k:2 * NB:2], T.y[0:32, 32 * k:32 * k + NB], float(MID), None, op.add), "listr")
+    vdep()
+    for q in range(1, 4):
+        vi(V.tensor_copy(T.lst[32 * q:32 * q + 32, 0:2 * NB], T.lst[0:32, 0:2 * NB]), "listr")
+
+    halves = (("a", T.psa, 0, HALF, HALF), ("b", T.psb, HALF, HALF, NP - HALF))
+
+    def product(ps, b, n, e, es, x, xs, at, start, stop):
+        return P.matmul_mx(ps[:, 512 * b:512 * b + n], e[:, 128 * b:128 * b + 128], es[:, 128 * b:128 * b + 128],
+                           x[:, at:at + n], xs[:, at:at + n], start, stop)
+
+    wait("p", P, "eq1", "wpc", "wps")
+    for name, ps, at, n, m in halves:
+        for b in range(4):
+            product(ps, b, n, T.q1, T.q1s, T.wsl, T.wsls, at, True, False)
+    wait("p", P, "eq2", "arc", "ownc", "ars", "owns")
+    vdep()
+    wait("v", V, "arc", "ownc")
+    wait("a", A, "listr", "ars", "owns")
+    for name, ps, at, n, m in halves:
+        off = T.lst[:, 2 * BF_ + at // 16:2 * BF_ + (at + m) // 16]
+        vi(V.tensor_copy(u32(T.pk[:, at:at + m]), u32(T.land[:, 0:NS + ZC]).indirect(off)), "pc" + name)
+        inc(A.activation(T.pks[:, at:at + m], T.lands[:, 0:NS + ZC].indirect(off), COPY), "pp" + name)
+    for name, ps, at, n, m in halves:
+        for b in range(4):
+            product(ps, b, n, T.q2, T.q2s, T.land, T.lands, at, False, False)
+        wait("p", P, "pc" + name, "pp" + name)
+        for b in range(4):
+            inc(product(ps, b, m, T.q2, T.q2s, T.pk, T.pks, at, False, True), "t%s%d" % (name, b))
+    vi(V.tensor_scalar(T.u0[0:32, :], T.sc[0:32, 0:BF_], 7.5 * NONE, None, op.is_lt))
+    vi(V.tensor_scalar(T.u1[0:32, :], T.sc[0:32, 0:BF_], 6.625 * NONE, None, op.is_lt))
+    vdep()
+    vi(V.tensor_tensor(T.ub[0:32, 0:BF_], T.u0[0:32, :], T.u1[0:32, :], op.add))
+    vdep()
+    vi(V.transpose(T.ut[0:32, :], T.ub[0:32, :]), "utr")
+
+    for name, ps, at, n, m in halves:
+        for b in range(4):
+            out, src = T.h[:, 4 * at + b:4 * (at + n):4], ps[:, 512 * b:512 * b + n]
+            if b % 2 == 0:
+                wait("v", V, "t%s%d" % (name, b))
+                vi(V.tensor_copy(out, src))
+            else:
+                wait("a", A, "t%s%d" % (name, b))
+                inc(A.activation(out, src, COPY), "hs" + name)
+        wait("v", V, "hs" + name)
+        vdep()
+        vi(V.quantize_mx(T.wn[:, at:at + n], T.wns[:, at:at + n], T.h[:, 4 * at:4 * (at + n)]), "qn" + name)
+
+    wait("v", V, "ldn")
+    vdep()
+    wait("a", A, "ldn", "qna", "qnb")
+    for k in range(2):
+        off = T.lst[:, 16 * k:16 * k + 16]
+        vi(V.tensor_copy(u32(T.on[:, 256 * k:256 * k + 256]), u32(T.wn[:, 0:NS + C]).indirect(off)), "onc%d" % k)
+        inc(A.activation(T.ons[:, 256 * k:256 * k + 256], T.wns[:, 0:NS + C].indirect(off), COPY), "ons%d" % k)
+    wait("y", Y, "utr")
+    inc(Y.dma_start(T.up[:], T.ut[0:16, :]), "st", 16)
+    for k in range(2):
+        wait("y", Y, "onc%d" % k)
+        inc(Y.dma_start(T.oc[:, 1024 * k:1024 * k + 1024], u8(T.on[:, 256 * k:256 * k + 256])), "st", 16)
+    for k in range(4):
+        qn, q = (("a", A), ("y", Y))[k // 2]
+        wait(qn, q, "ons0", "ons1")
+        inc(q.dma_start(T.osc[4 * k:4 * k + 4, :], T.ons[32 * k:32 * k + 4, :]), "st", 16)
+
+    for name in total:
+        if name not in ("st",):
+            wait("g", g, name)
+    wait("y", Y, "st")

@@ -5,18 +5,22 @@ X4, U8 = "float8_e4m3fn_x4", "uint8"
 C, S, CAPP, N = 512, 256, 48, 8
 NS = N * CAPP
 HALF = NS // 2
-ZC = 128
+ZC = 2
 NP = NS - CAPP
 NV = 352
-FW = C + 160
+W0 = 16
+FW = W0 + C + 176
 MID, NONE = 192, 768
 LC = NS // 16
+LV = NV // 16
+ST = 6
 BF_, BV = C // 32, NV // 32
 NB = BF_ + BV
+EW = 520
 
 SCRATCH = {
     "grt": ("sbuf", [128, 4 * S], "bfloat16"),
-    "sni": ("sbuf", [128, LC], "int32"), "tci": ("sbuf", [128, 28], "int32"),
+    "sni": ("sbuf", [128, LC], "int32"), "tci": ("sbuf", [128, LC], "int32"),
     "soff": ("sbuf", [128, LC], "uint16"), "woff": ("sbuf", [128, LC], "uint16"),
     "gq": ("sbuf", [128, S], X4), "gqs": ("sbuf", [128, S], U8),
     "gp": ("sbuf", [128, NS], X4), "gps": ("sbuf", [128, NS], U8),
@@ -26,28 +30,29 @@ SCRATCH = {
     "pk": ("sbuf", [128, NS], X4), "pks": ("sbuf", [128, NS], U8),
     "wn": ("sbuf", [128, NS + C], X4), "wns": ("sbuf", [128, NS + C], U8),
     "on": ("sbuf", [128, C], X4), "ons": ("sbuf", [128, C], U8),
-    "zer": ("sbuf", [128, 516], "bfloat16"), "eb": ("sbuf", [128, 516], "bfloat16"), "e2": ("sbuf", [128, 516], "bfloat16"),
-    "q1": ("sbuf", [128, 512], X4), "q1s": ("sbuf", [128, 512], U8),
+    "eb": ("sbuf", [128, EW], "bfloat16"), "e2": ("sbuf", [128, EW], "bfloat16"),
+    "q1": ("sbuf", [128, 512 + ZC], X4), "q1s": ("sbuf", [128, 512 + ZC], U8),
     "q2": ("sbuf", [128, 512], X4), "q2s": ("sbuf", [128, 512], U8),
-    "k1": ("sbuf", [128, 28], "int32"), "t2": ("sbuf", [128, 28], "int32"), "t3": ("sbuf", [128, 28], "int32"),
-    "toff": ("sbuf", [128, 28], "uint16"),
+    "pn": ("sbuf", [128, 2], "int32"), "ooff": ("sbuf", [128, 2], "uint16"),
+    "kl": ("sbuf", [128, LC], "int32"), "ko": ("sbuf", [128, 16], "int32"),
+    "t2": ("sbuf", [128, LC], "int32"), "t3": ("sbuf", [128, ST * LV + 16], "int32"),
+    "toff": ("sbuf", [128, LV + 4], "uint16"),
     "vals": ("sbuf", [128, CAPP], "bfloat16"),
     "fb": ("sbuf", [128, FW], "bfloat16"),
     "vv": ("sbuf", [128, NV], "bfloat16"),
     "tt": ("sbuf", [128, C + NV], "bfloat16"),
-    "sa": ("sbuf", [128, 32], "float32"), "sb": ("sbuf", [128, 32], "float32"), "sc": ("sbuf", [128, 32], "float32"),
-    "ma": ("sbuf", [128, 16], "float32"), "mb": ("sbuf", [128, 16], "float32"), "mc": ("sbuf", [128, 16], "float32"),
-    "kf": ("sbuf", [128, 16], "float32"), "kv": ("sbuf", [128, 16], "float32"), "dv": ("sbuf", [128, 16], "float32"),
-    "r": ("sbuf", [128, 32], "float32"), "z": ("sbuf", [128, 64], "float32"), "y": ("sbuf", [128, 64], "float32"),
+    "ma": ("sbuf", [128, 32], "float32"), "mb": ("sbuf", [128, 32], "float32"),
+    "kf": ("sbuf", [128, 16], "float32"),
+    "r": ("sbuf", [128, 64], "float32"), "z": ("sbuf", [128, 64], "float32"), "y": ("sbuf", [128, 64], "float32"),
     "lst": ("sbuf", [128, 64], "uint16"),
-    "u0": ("sbuf", [128, 16], "float32"), "u1": ("sbuf", [128, 16], "float32"),
-    "ub": ("sbuf", [128, 32], "float32"), "ut": ("sbuf", [128, 32], "float32"),
+    "u0": ("sbuf", [128, 32], "float32"), "u1": ("sbuf", [128, 16], "float32"), "u2": ("sbuf", [128, 16], "float32"),
+    "ut": ("sbuf", [128, 32], "float32"),
     "h": ("sbuf", [128, 4 * NS], "bfloat16"),
     "psa": ("psum", [128, 2048], "float32"), "psb": ("psum", [128, 2048], "float32"),
 }
-SEMAPHORES = ["ldg", "lds", "ldt", "ldw", "ldn", "ownc", "owns", "st", "arc", "ars", "sent", "v", "z", "gi", "ea", "e2r", "eq1", "eq2", "soffr", "gqr", "gpc", "gpp",
-              "woffr", "tof", "fg", "vg", "wpc", "wps", "listr", "utr", "ons0", "ons1", "onc0", "onc1"] + \
-             [k + h for k in ("pc", "pp", "hs", "qn") for h in "ab"] + ["t%s%d" % (h, b) for h in "ab" for b in range(4)]
+SEMAPHORES = ["ldg", "lds", "ldt", "ldw", "ldn", "ownc", "owns", "st", "arc", "ars", "sent", "v", "z1", "z2", "fill", "gp0", "gi", "ea", "e2r",
+              "eq1", "eq2", "soffr", "gqr", "gpc", "gpp", "woffr", "tof", "fg", "vg", "listr", "utr", "ons0", "onc0", "onc1"] + \
+             [k + h for k in ("wc", "wp", "pc", "pp", "hs", "qn") for h in "ab"] + ["t%s%d" % (h, b) for h in "ab" for b in range(4)]
 
 
 def rank_program(g, core, T, topo):
@@ -56,9 +61,9 @@ def rank_program(g, core, T, topo):
         return
     V, P, A, Y = g.vector, g.tensor, g.scalar, g.sync
     COPY = ActivationFunctionType.Copy
-    total, seen, mine = {}, {}, {}
+    total, seen = {}, {}
 
-    def inc(ins, name, n=1):
+    def inc(ins, name="v", n=1):
         ins.then_inc(T.sem[name], n)
         total[name] = total.get(name, 0) + n
         return name
@@ -69,12 +74,8 @@ def rank_program(g, core, T, topo):
                 q.wait_ge(T.sem[name], total[name])
                 seen[(qn, name)] = total[name]
 
-    def vi(ins, name="v"):
-        mine[inc(ins, name)] = 1
-
-    def vdep():
-        wait("v", V, *sorted(mine))
-        mine.clear()
+    def vw(*evs):
+        wait("v", V, *(evs or ("v",)))
 
     def u8(v):
         return v.bitcast(dt.uint8)
@@ -82,42 +83,48 @@ def rank_program(g, core, T, topo):
     def u32(v):
         return v.bitcast(dt.uint32)
 
-    inc(Y.dma_start(T.grt[:, 0:2 * S], T.gr[:, 0:2 * S]), "ldg", 16)
-    inc(A.dma_start(T.grt[:, 2 * S:4 * S], T.gr[:, 2 * S:4 * S]), "ldg", 16)
-    for k in range(N):
-        inc((Y, A)[k % 2].dma_start(T.sni[16 * k:16 * k + 16, :], T.sn[:]), "lds", 16)
-    for k in range(N):
-        inc((Y, A)[k % 2].dma_start(T.tci[16 * k:16 * k + 16, 0:LC], T.tc[:]), "ldt", 16)
-    for k in range(N):
-        inc(Y.dma_start(T.tci[16 * k:16 * k + 16, LC:LC + 3], T.tc[:, 3 * k:3 * k + 3]), "ldt", 16)
+    inc(Y.dma_start(T.grt[:], T.gr[:]), "ldg", 16)
+    for k, q in enumerate((A, Y, A, A)):
+        inc(q.dma_start(T.sni[16 * k:16 * k + 16, :], T.sn[:]), "lds", 16)
+    for k, q in enumerate((Y, A)):
+        inc(q.dma_start(T.tci[16 * k:16 * k + 16, :], T.tc[:]), "ldt", 16)
     inc(Y.dma_start(u8(T.w2[:]), T.wc[:]), "ldw", 16)
     inc(A.dma_start(T.w2s[:], T.ws[:]), "ldw", 16)
 
     F32 = {"allow_small_or_imprecise_dtypes": True}
-    vi(V.memset(T.zer[:], 0.0), "z")
-    inc(g.iota(T.k1[:, 0:LC + 3], [[0, N + 1], [16, 3]], C, 1), "gi")
-    wait("g", g, "z")
-    inc(g.affine_select(T.eb[:], T.zer[:], [[1, 516]], op.not_equal, 1.0, -3, -4), "ea")
+    inc(V.memset(T.eb[:], 0.0), "z1")
+    inc(V.memset(T.e2[:], 0.0), "z2")
+    inc(g.iota(T.pn[:], [[0, 2]], 0, 1), "gp0")
+    for e, zz, fill, name in ((T.eb, "z1", 1.0, "ea"), (T.e2, "z2", -0.125, "e2r")):
+        wait("g", g, zz)
+        inc(g.affine_select(e[:, 3:515:4], e[:, 3:515:4], [[1, 128]], op.not_equal, fill, 0, -1), name)
+    inc(g.iota(T.kl[:], [[-9600, N], [0, 3]], -9040, 600), "gi")
+    inc(g.iota(T.ko[:], [[3, 16]], C, 1), "gi")
     inc(g.iota(T.vals[:], [[1, CAPP]], -MID, 3, **F32), "gi")
     inc(g.iota(T.kf[0:32, :], [[32, BF_]], NS - MID, 1, **F32), "gi")
-    inc(g.iota(T.kv[0:32, 0:BV], [[32, BV]], 6 * NONE - MID, 1, **F32), "gi")
-    vi(V.memset(T.fb[:], float(NONE)))
-    vi(V.memset(T.r[:], 0.0))
-    vi(V.memset(T.ub[:], 0.0))
-    vdep()
-    vi(V.quantize_mx(T.land[:, NS:NS + ZC], T.lands[:, NS:NS + ZC], T.zer[:, 0:4 * ZC]))
-    wait("a", A, "ea")
-    inc(A.activation(T.e2[:], T.eb[:], COPY, scale=-0.125), "e2r")
-    wait("v", V, "ea")
+    inc(V.memset(T.fb[:, 0:W0], float(NS - MID)), "fill")
+    inc(V.memset(T.fb[:, W0:FW], float(NONE)), "fill")
+    inc(V.memset(T.r[:], 0.0), "fill")
+    vw("gp0")
+    inc(V.tensor_scalar(T.ooff[:], T.pn[:], 3 / 16, float(LC - 1), op.mult, op.min), "fill")
+    vw("ea")
     for b in range(4):
-        vi(V.quantize_mx(T.q1[:, 128 * b:128 * b + 128], T.q1s[:, 128 * b:128 * b + 128], T.eb[:, 3 - b:515 - b]), "eq1")
+        n = 128 + ZC * (b == 3)
+        inc(V.quantize_mx(T.q1[:, 128 * b:128 * b + n], T.q1s[:, 128 * b:128 * b + n], T.eb[:, 3 - b:3 - b + 4 * n]), "eq1")
+    vw("e2r")
+    for b in range(4):
+        inc(V.quantize_mx(T.q2[:, 128 * b:128 * b + 128], T.q2s[:, 128 * b:128 * b + 128], T.e2[:, 3 - b:515 - b]), "eq2")
+    wait("y", Y, "eq1")
+    inc(Y.dma_start(u8(T.land[:, NS:NS + ZC]), u8(T.q1[:, 512:512 + ZC])), "ownc", 16)
+    inc(Y.dma_start(T.lands[:, NS:NS + ZC], T.q1s[:, 512:512 + ZC]), "owns", 16)
 
-    wait("v", V, "lds")
-    vi(V.tensor_copy(T.soff[:], T.sni[:]), "soffr")
-    wait("v", V, "ldg")
-    vi(V.quantize_mx(T.gq[:], T.gqs[:], T.grt[:]), "gqr")
-    vdep()
-    vi(V.tensor_copy(u32(T.gp[:, 0:NS]), u32(T.gq[:, 0:S]).indirect(T.soff[:])), "gpc")
+    vw("ldg")
+    inc(V.quantize_mx(T.gq[:], T.gqs[:], T.grt[:]), "gqr")
+    vw("lds")
+    for k in range(2):
+        inc(V.tensor_copy(T.soff[64 * k:64 * k + 64, :], T.sni[0:64, :]), "soffr")
+    vw("gqr", "soffr")
+    inc(V.tensor_copy(u32(T.gp[:, 0:NS]), u32(T.gq[:, 0:S]).indirect(T.soff[:])), "gpc")
     wait("a", A, "soffr", "gqr")
     inc(A.activation(T.gps[:, 0:NS], T.gqs[:, 0:S].indirect(T.soff[:]), COPY), "gpp")
 
@@ -150,117 +157,110 @@ def rank_program(g, core, T, topo):
     inc(Y.dma_start(u8(T.wn[:, NS:NS + C]), T.wc[:]), "ldn", 16)
     inc(Y.dma_start(T.wns[:, NS:NS + C], T.ws[:]), "ldn", 16)
 
-    wait("v", V, "ldt", "gi")
-    vi(V.tensor_scalar(T.t2[:, 0:LC + 3], T.tci[:, 0:LC + 3], 1023, None, op.bitwise_and))
-    vi(V.tensor_copy(T.woff[:], T.tci[:, 0:LC]), "woffr")
-    vdep()
-    vi(V.tensor_tensor(T.t3[:, 0:LC + 3], T.t2[:, 0:LC + 3], T.k1[:, 0:LC + 3], op.min))
-    vdep()
-    vi(V.tensor_copy(T.toff[:, 0:LC + 3], T.t3[:, 0:LC + 3]), "tof")
-    vdep()
-    vi(V.tensor_copy(T.fb[:, 0:FW].indirect(T.toff[:, LC:LC + 3]), T.vals[:]), "fg")
-    wait("a", A, "fg", "tof")
-    inc(A.activation(T.vv[:], T.fb[:, 0:FW].indirect(T.toff[:, 0:NV // 16]), COPY), "vg")
-    wait("a", A, "woffr", "ldw")
-    inc(A.activation(T.wsls[:], T.w2s[:, 0:C].indirect(T.woff[:]), COPY), "wps")
-    wait("v", V, "e2r")
-    for b in range(4):
-        vi(V.quantize_mx(T.q2[:, 128 * b:128 * b + 128], T.q2s[:, 128 * b:128 * b + 128], T.e2[:, 3 - b:515 - b]), "eq2")
-    wait("v", V, "ldw")
-    vi(V.tensor_copy(u32(T.wsl[:]), u32(T.w2[:, 0:C]).indirect(T.woff[:])), "wpc")
-    wait("v", V, "fg")
-    vi(V.transpose(T.tt[:, 0:C], T.fb[:, 0:C]))
-    wait("v", V, "vg")
-    vi(V.transpose(T.tt[:, C:C + NV], T.vv[:]))
-    vdep()
-    vi(V.tensor_tensor(T.ma[:], T.tt[:, 0:C:32], T.tt[:, 16:C:32], op.min))
-    vi(V.tensor_tensor(T.sa[:, 0:NB], T.tt[:, 0:C + NV:32], T.tt[:, 16:C + NV:32], op.add))
-    vdep()
-    vi(V.tensor_tensor(T.mb[0:64, :], T.ma[0:64, :], T.ma[64:128, :], op.min))
-    vdep()
-    vi(V.tensor_tensor(T.sb[0:64, 0:NB], T.sa[0:64, 0:NB], T.sa[64:128, 0:NB], op.add))
-    vdep()
-    vi(V.tensor_tensor(T.mc[0:32, :], T.mb[0:32, :], T.mb[32:64, :], op.min))
-    vdep()
-    vi(V.tensor_tensor(T.sc[0:32, 0:NB], T.sb[0:32, 0:NB], T.sb[32:64, 0:NB], op.add))
-    vdep()
-    vi(V.tensor_tensor(T.dv[0:32, 0:BV], T.sc[0:32, BF_:NB], T.kv[0:32, 0:BV], op.subtract))
-    vi(V.tensor_tensor(T.r[0:32, 0:BF_], T.mc[0:32, :], T.kf[0:32, :], op.min))
-    vdep()
-    vi(V.tensor_scalar(T.r[0:32, BF_:NB], T.dv[0:32, 0:BV], float(NS - MID), None, op.min))
-    vdep()
-    vi(V.transpose(T.z[0:32, 16:48], T.r[0:32, :]))
-    vdep()
-    vi(V.tensor_copy(T.z[0:32, 0:16], T.z[0:32, 16:32]))
-    vi(V.tensor_copy(T.z[0:32, 48:64], T.z[0:32, 32:48]))
-    vdep()
-    vi(V.transpose(T.y[0:32, :], T.z[0:32, :]))
-    vdep()
-    for k in range(2):
-        vi(V.tensor_scalar(T.lst[0:32, k:2 * NB:2], T.y[0:32, 32 * k:32 * k + NB], float(MID), None, op.add), "listr")
-    vdep()
-    for q in range(1, 4):
-        vi(V.tensor_copy(T.lst[32 * q:32 * q + 32, 0:2 * NB], T.lst[0:32, 0:2 * NB]), "listr")
+    vw("ldt")
+    for q in range(4):
+        inc(V.tensor_scalar(T.t2[32 * q:32 * q + 32, :], T.tci[0:32, :], 1023, None, op.bitwise_and))
+    vw("v", "gi", "fill")
+    inc(V.tensor_tensor(T.t3[:, ST * LV:ST * LV + 16], T.t2[:, 0:LC].indirect(T.ooff[:, 0:1]), T.ko[:], op.min))
+    inc(V.tensor_tensor(T.t3[:, 0:ST * LV:ST], T.t2[:, 0:LV], T.kl[:, 0:LV], op.min))
+    inc(V.tensor_scalar(T.woff[:], T.t2[:], float(C - 1), None, op.min), "woffr")
+    vw()
+    inc(V.tensor_scalar(T.toff[:, 0:LV + 3], T.t3[:, 0:ST * (LV + 2) + 1:ST], float(W0), float(FW - 1), op.add, op.min), "tof")
+    vw("tof")
+    inc(V.tensor_copy(T.fb[:, 0:FW].indirect(T.toff[:, LV:LV + 3]), T.vals[:]), "fg")
 
     halves = (("a", T.psa, 0, HALF, HALF), ("b", T.psb, HALF, HALF, NP - HALF))
+    vw("woffr", "ldw")
+    wait("a", A, "woffr", "ldw")
+    for name, ps, at, n, m in halves:
+        off = T.woff[:, at // 16:(at + n) // 16]
+        inc(V.tensor_copy(u32(T.wsl[:, at:at + n]), u32(T.w2[:, 0:C]).indirect(off)), "wc" + name)
+        inc(A.activation(T.wsls[:, at:at + n], T.w2s[:, 0:C].indirect(off), COPY), "wp" + name)
+        if name == "a":
+            wait("a", A, "fg", "tof")
+            inc(A.activation(T.vv[:], T.fb[:, 0:FW].indirect(T.toff[:, 0:LV]), COPY), "vg")
+    vw("fg")
+    inc(V.transpose(T.tt[:, 0:C], T.fb[:, W0:W0 + C]))
+    vw("vg")
+    inc(V.transpose(T.tt[:, C:C + NV], T.vv[:]))
+    vw()
+    inc(V.tensor_tensor(T.ma[:, 0:NB], T.tt[:, 0:C + NV:32], T.tt[:, 16:C + NV:32], op.min))
+    vw()
+    inc(V.tensor_tensor(T.mb[0:64, 0:NB], T.ma[0:64, 0:NB], T.ma[64:128, 0:NB], op.min))
+    vw()
+    inc(V.tensor_tensor(T.r[0:32, 0:NB], T.mb[0:32, 0:NB], T.mb[32:64, 0:NB], op.min))
+    vw()
+    inc(V.tensor_tensor(T.r[0:32, 0:BF_], T.r[0:32, 0:BF_], T.kf[0:32, :], op.min))
+    vw()
+    inc(V.transpose(T.z[0:32, 16:48], T.r[0:32, 0:32]))
+    vw()
+    inc(V.tensor_copy(T.z[0:32, 0:16], T.z[0:32, 16:32]))
+    inc(V.tensor_copy(T.z[0:32, 48:64], T.z[0:32, 32:48]))
+    vw()
+    for k in range(2):
+        inc(V.transpose(T.y[0:32, k:64:2], T.z[0:32, 32 * k:32 * k + 32]))
+    vw()
+    for q in range(4):
+        inc(V.tensor_scalar(T.lst[32 * q:32 * q + 32, 0:2 * NB], T.y[0:32, 0:2 * NB], float(MID), None, op.add), "listr")
 
     def product(ps, b, n, e, es, x, xs, at, start, stop):
         return P.matmul_mx(ps[:, 512 * b:512 * b + n], e[:, 128 * b:128 * b + 128], es[:, 128 * b:128 * b + 128],
                            x[:, at:at + n], xs[:, at:at + n], start, stop)
 
-    wait("p", P, "eq1", "wpc", "wps")
+    wait("p", P, "eq1")
     for name, ps, at, n, m in halves:
+        wait("p", P, "wc" + name, "wp" + name)
         for b in range(4):
             product(ps, b, n, T.q1, T.q1s, T.wsl, T.wsls, at, True, False)
     wait("p", P, "eq2", "arc", "ownc", "ars", "owns")
-    vdep()
-    wait("v", V, "arc", "ownc")
-    wait("a", A, "listr", "ars", "owns")
-    for name, ps, at, n, m in halves:
-        off = T.lst[:, 2 * BF_ + at // 16:2 * BF_ + (at + m) // 16]
-        vi(V.tensor_copy(u32(T.pk[:, at:at + m]), u32(T.land[:, 0:NS + ZC]).indirect(off)), "pc" + name)
-        inc(A.activation(T.pks[:, at:at + m], T.lands[:, 0:NS + ZC].indirect(off), COPY), "pp" + name)
     for name, ps, at, n, m in halves:
         for b in range(4):
             product(ps, b, n, T.q2, T.q2s, T.land, T.lands, at, False, False)
+    vw("listr", "arc", "ownc")
+    wait("a", A, "listr", "ars", "owns")
+    for name, ps, at, n, m in halves:
+        off = T.lst[:, 2 * BF_ + at // 16:2 * BF_ + (at + m) // 16]
+        inc(V.tensor_copy(u32(T.pk[:, at:at + m]), u32(T.land[:, 0:NS + ZC]).indirect(off)), "pc" + name)
+        inc(A.activation(T.pks[:, at:at + m], T.lands[:, 0:NS + ZC].indirect(off), COPY), "pp" + name)
         wait("p", P, "pc" + name, "pp" + name)
         for b in range(4):
             inc(product(ps, b, m, T.q2, T.q2s, T.pk, T.pks, at, False, True), "t%s%d" % (name, b))
-    vi(V.tensor_scalar(T.u0[0:32, :], T.sc[0:32, 0:BF_], 7.5 * NONE, None, op.is_lt))
-    vi(V.tensor_scalar(T.u1[0:32, :], T.sc[0:32, 0:BF_], 6.625 * NONE, None, op.is_lt))
-    vdep()
-    vi(V.tensor_tensor(T.ub[0:32, 0:BF_], T.u0[0:32, :], T.u1[0:32, :], op.add))
-    vdep()
-    vi(V.transpose(T.ut[0:32, :], T.ub[0:32, :]), "utr")
+    inc(V.tensor_scalar(T.u0[:], T.tt[:, 0:C:16], float(C), None, op.is_lt))
+    vw()
+    inc(V.tensor_tensor(T.u1[:], T.u0[:, 0:32:2], T.u0[:, 1:32:2], op.add))
+    vw()
+    inc(V.tensor_tensor(T.u2[0:64, :], T.u1[0:64, :], T.u1[64:128, :], op.add))
+    vw()
+    inc(V.tensor_tensor(T.r[0:32, 32:32 + BF_], T.u2[0:32, :], T.u2[32:64, :], op.add))
+    vw()
+    inc(V.transpose(T.ut[0:32, :], T.r[0:32, 32:64]), "utr")
 
     for name, ps, at, n, m in halves:
         for b in range(4):
             out, src = T.h[:, 4 * at + b:4 * (at + n):4], ps[:, 512 * b:512 * b + n]
             if b % 2 == 0:
-                wait("v", V, "t%s%d" % (name, b))
-                vi(V.tensor_copy(out, src))
+                vw("t%s%d" % (name, b))
+                inc(V.tensor_copy(out, src))
             else:
                 wait("a", A, "t%s%d" % (name, b))
                 inc(A.activation(out, src, COPY), "hs" + name)
-        wait("v", V, "hs" + name)
-        vdep()
-        vi(V.quantize_mx(T.wn[:, at:at + n], T.wns[:, at:at + n], T.h[:, 4 * at:4 * (at + n)]), "qn" + name)
+        vw("v", "hs" + name)
+        inc(V.quantize_mx(T.wn[:, at:at + n], T.wns[:, at:at + n], T.h[:, 4 * at:4 * (at + n)]), "qn" + name)
 
-    wait("v", V, "ldn")
-    vdep()
+    vw("ldn", "qna", "qnb")
     wait("a", A, "ldn", "qna", "qnb")
     for k in range(2):
         off = T.lst[:, 16 * k:16 * k + 16]
-        vi(V.tensor_copy(u32(T.on[:, 256 * k:256 * k + 256]), u32(T.wn[:, 0:NS + C]).indirect(off)), "onc%d" % k)
-        inc(A.activation(T.ons[:, 256 * k:256 * k + 256], T.wns[:, 0:NS + C].indirect(off), COPY), "ons%d" % k)
+        inc(V.tensor_copy(u32(T.on[:, 256 * k:256 * k + 256]), u32(T.wn[:, 0:NS + C]).indirect(off)), "onc%d" % k)
+    inc(A.activation(T.ons[:], T.wns[:, 0:NS + C].indirect(T.lst[:, 0:32]), COPY), "ons0")
     wait("y", Y, "utr")
     inc(Y.dma_start(T.up[:], T.ut[0:16, :]), "st", 16)
     for k in range(2):
         wait("y", Y, "onc%d" % k)
         inc(Y.dma_start(T.oc[:, 1024 * k:1024 * k + 1024], u8(T.on[:, 256 * k:256 * k + 256])), "st", 16)
     for k in range(4):
-        qn, q = (("a", A), ("y", Y))[k // 2]
-        wait(qn, q, "ons0", "ons1")
+        qn, q = (("a", A), ("y", Y))[k // 3]
+        wait(qn, q, "ons0")
         inc(q.dma_start(T.osc[4 * k:4 * k + 4, :], T.ons[32 * k:32 * k + 4, :]), "st", 16)
 
     for name in total:

@@ -1,6 +1,7 @@
 from concourse.bass import DstId, RemoteDMATransfer
 from concourse.mybir import dt, AluOpType as op, ActivationFunctionType
 
+CHUNKS = (18, 14)
 X4, U8 = "float8_e4m3fn_x4", "uint8"
 C, S, CAPP, N = 512, 256, 48, 8
 NS = N * CAPP
@@ -42,17 +43,26 @@ SCRATCH = {
     "vv": ("sbuf", [128, NV], "bfloat16"),
     "tt": ("sbuf", [128, C + NV], "bfloat16"),
     "ma": ("sbuf", [128, 32], "float32"), "mb": ("sbuf", [128, 32], "float32"),
-    "kf": ("sbuf", [128, 16], "float32"),
-    "r": ("sbuf", [128, 64], "float32"), "z": ("sbuf", [128, 64], "float32"), "y": ("sbuf", [128, 64], "float32"),
+    "kf": ("sbuf", [128, 16], "float32"), "ta": ("sbuf", [128, 16], "float32"),
+    "r": ("sbuf", [128, 64], "float32"), "z": ("sbuf", [128, 4, 16], "float32"), "y": ("sbuf", [128, 64], "float32"),
     "lst": ("sbuf", [128, 64], "uint16"),
     "u0": ("sbuf", [128, 32], "float32"), "u1": ("sbuf", [128, 16], "float32"), "u2": ("sbuf", [128, 16], "float32"),
     "ut": ("sbuf", [128, 32], "float32"),
     "h": ("sbuf", [128, 4 * NS], "bfloat16"),
     "psa": ("psum", [128, 2048], "float32"), "psb": ("psum", [128, 2048], "float32"),
 }
-SEMAPHORES = ["ldg", "lds", "ldt", "ldw", "ldn", "ownc", "owns", "st", "arc", "ars", "sent", "v", "z1", "z2", "fill", "gp0", "gi", "ea", "e2r",
-              "eq1", "eq2", "soffr", "gqr", "gpc", "gpp", "woffr", "tof", "fg", "vg", "listr", "utr", "ons0", "onc0", "onc1"] + \
-             [k + h for k in ("wc", "wp", "pc", "pp", "hs", "qn") for h in "ab"] + ["t%s%d" % (h, b) for h in "ab" for b in range(4)]
+SEMAPHORES = ["ldg0", "ldg1", "gpc0", "gpc1", "gpp0", "gpp1", "arc0", "arc1", "ars0", "ars1", "tf", "cnt", "hsa", "hsb", "lds", "ldt", "ldw", "ldn", "ownc", "owns", "st", "sent", "v", "z1", "z2", "fill", "gp0", "gi", "ea", "e2r",
+              "eq1", "eq2", "soffr", "gqr", "woffr", "tof", "fg", "vg", "listr", "utr", "qn", "ons0"] + \
+             ["onc%d" % k for k in range(len(CHUNKS))] + \
+             [k + h for k in ("wc", "wp", "pc", "pp") for h in "ab"] + ["t%s%d" % (h, b) for h in "ab" for b in range(4)]
+
+
+def u8(v):
+    return v.bitcast(dt.uint8)
+
+
+def u32(v):
+    return v.bitcast(dt.uint32)
 
 
 def rank_program(g, core, T, topo):
@@ -77,16 +87,11 @@ def rank_program(g, core, T, topo):
     def vw(*evs):
         wait("v", V, *(evs or ("v",)))
 
-    def u8(v):
-        return v.bitcast(dt.uint8)
-
-    def u32(v):
-        return v.bitcast(dt.uint32)
-
-    inc(Y.dma_start(T.grt[:], T.gr[:]), "ldg", 16)
-    for k, q in enumerate((A, Y, A, A)):
-        inc(q.dma_start(T.sni[16 * k:16 * k + 16, :], T.sn[:]), "lds", 16)
-    for k, q in enumerate((Y, A)):
+    for k in range(2):
+        inc(Y.dma_start(T.grt[:, 2 * S * k:2 * S * (k + 1)], T.gr[:, 2 * S * k:2 * S * (k + 1)]), "ldg%d" % k, 16)
+    for k in range(4):
+        inc(A.dma_start(T.sni[16 * k:16 * k + 16, :], T.sn[:]), "lds", 16)
+    for k, q in enumerate((Y, Y, Y, A)):
         inc(q.dma_start(T.tci[16 * k:16 * k + 16, :], T.tc[:]), "ldt", 16)
     inc(Y.dma_start(u8(T.w2[:]), T.wc[:]), "ldw", 16)
     inc(A.dma_start(T.w2s[:], T.ws[:]), "ldw", 16)
@@ -101,7 +106,7 @@ def rank_program(g, core, T, topo):
     inc(g.iota(T.kl[:], [[-9600, N], [0, 3]], -9040, 600), "gi")
     inc(g.iota(T.ko[:], [[3, 16]], C, 1), "gi")
     inc(g.iota(T.vals[:], [[1, CAPP]], -MID, 3, **F32), "gi")
-    inc(g.iota(T.kf[0:32, :], [[32, BF_]], NS - MID, 1, **F32), "gi")
+    inc(g.iota(T.kf[:], [[32, BF_]], NS - MID, 1, **F32), "gi")
     inc(V.memset(T.fb[:, 0:W0], float(NS - MID)), "fill")
     inc(V.memset(T.fb[:, W0:FW], float(NONE)), "fill")
     inc(V.memset(T.r[:], 0.0), "fill")
@@ -111,55 +116,57 @@ def rank_program(g, core, T, topo):
     for b in range(4):
         n = 128 + ZC * (b == 3)
         inc(V.quantize_mx(T.q1[:, 128 * b:128 * b + n], T.q1s[:, 128 * b:128 * b + n], T.eb[:, 3 - b:3 - b + 4 * n]), "eq1")
-    vw("e2r")
-    for b in range(4):
-        inc(V.quantize_mx(T.q2[:, 128 * b:128 * b + 128], T.q2s[:, 128 * b:128 * b + 128], T.e2[:, 3 - b:515 - b]), "eq2")
     wait("y", Y, "eq1")
     inc(Y.dma_start(u8(T.land[:, NS:NS + ZC]), u8(T.q1[:, 512:512 + ZC])), "ownc", 16)
     inc(Y.dma_start(T.lands[:, NS:NS + ZC], T.q1s[:, 512:512 + ZC]), "owns", 16)
 
-    vw("ldg")
-    inc(V.quantize_mx(T.gq[:], T.gqs[:], T.grt[:]), "gqr")
+    vw("e2r")
+    for b in range(4):
+        inc(V.quantize_mx(T.q2[:, 128 * b:128 * b + 128], T.q2s[:, 128 * b:128 * b + 128], T.e2[:, 3 - b:515 - b]), "eq2")
+
+    lo = CAPP * rank
     vw("lds")
     for k in range(2):
         inc(V.tensor_copy(T.soff[64 * k:64 * k + 64, :], T.sni[0:64, :]), "soffr")
+    for k in range(2):
+        vw("ldg%d" % k)
+        inc(V.quantize_mx(T.gq[:, 128 * k:128 * k + 128], T.gqs[:, 128 * k:128 * k + 128], T.grt[:, 2 * S * k:2 * S * (k + 1)]), "gqr")
     vw("gqr", "soffr")
-    inc(V.tensor_copy(u32(T.gp[:, 0:NS]), u32(T.gq[:, 0:S]).indirect(T.soff[:])), "gpc")
     wait("a", A, "soffr", "gqr")
-    inc(A.activation(T.gps[:, 0:NS], T.gqs[:, 0:S].indirect(T.soff[:]), COPY), "gpp")
-
-    dests = [(rank + k) % N for k in range(1, N)]
-    lo = CAPP * rank
-
-    def transfers(scales):
-        out = []
-        for k, q in enumerate(dests):
-            d = T.cores[q]
-            rid, pid = topo.addr(d, core)
-            a = CAPP * q
-            src = T.gps[:, a:a + CAPP] if scales else u8(T.gp[:, a:a + CAPP])
-            dst = T.lands[:, lo:lo + CAPP] if scales else u8(T.land[:, lo:lo + CAPP])
-            out.append(RemoteDMATransfer(dst_ids=[DstId(rid=rid, pnc=pid)], dma_engine_mask=1 << topo.engines(core, d)[k],
-                                         remote_sem=T.sem.ars if scales else T.sem.arc, src=src, dst=dst))
-        return out
-
-    wait("g", g, "gpc")
-    g.remote_dma_fused(transfers(False), local_sem=T.sem.sent)
-    wait("g", g, "gpp")
-    g.remote_dma_fused(transfers(True), local_sem=T.sem.sent)
-    total["sent"] = 2 * len(dests)
-    total["arc"] = total["ars"] = len(dests)
-    wait("y", Y, "gpc")
+    H = N // 2
+    mine = rank // H
+    total["sent"] = 0
+    for wave, hf in enumerate((1 - mine, mine)):
+        off = T.soff[:, LC // 2 * hf:LC // 2 * (hf + 1)]
+        inc(V.tensor_copy(u32(T.gp[:, HALF * hf:HALF * (hf + 1)]), u32(T.gq[:, 0:S]).indirect(off)), "gpc%d" % wave)
+        inc(A.activation(T.gps[:, HALF * hf:HALF * (hf + 1)], T.gqs[:, 0:S].indirect(off), COPY), "gpp%d" % wave)
+        dests = [H * hf + (rank + k) % H for k in range(wave, H)]
+        shares = ([(0, 1), (2, 3), (4, 5), (6, 7)], [(0, 2, 4, 6), (1, 3), (5, 7)])[wave]
+        for scales in (False, True):
+            out, sem = [], ("ars%d" if scales else "arc%d") % wave
+            for q, share in zip(dests, shares):
+                d = T.cores[q]
+                rid, pid = topo.addr(d, core)
+                a = CAPP * q
+                src = T.gps[:, a:a + CAPP] if scales else u8(T.gp[:, a:a + CAPP])
+                dst = T.lands[:, lo:lo + CAPP] if scales else u8(T.land[:, lo:lo + CAPP])
+                out.append(RemoteDMATransfer(dst_ids=[DstId(rid=rid, pnc=pid)], dma_engine_mask=sum(1 << topo.engines(core, d)[e] for e in share),
+                                             remote_sem=T.sem[sem], src=src, dst=dst))
+            wait("g", g, ("gpp%d" if scales else "gpc%d") % wave)
+            g.remote_dma_fused(out, local_sem=T.sem.sent)
+            total[sem] = sum(len(share) for share in shares)
+            total["sent"] += total[sem]
+    wait("y", Y, "gpc1")
     inc(Y.dma_start(u8(T.land[:, lo:lo + CAPP]), u8(T.gp[:, lo:lo + CAPP])), "ownc", 16)
-    wait("y", Y, "gpp")
+    wait("y", Y, "gpp1")
     inc(Y.dma_start(T.lands[:, lo:lo + CAPP], T.gps[:, lo:lo + CAPP]), "owns", 16)
     wait("y", Y, "sent")
     inc(Y.dma_start(u8(T.wn[:, NS:NS + C]), T.wc[:]), "ldn", 16)
     inc(Y.dma_start(T.wns[:, NS:NS + C], T.ws[:]), "ldn", 16)
 
     vw("ldt")
-    for q in range(4):
-        inc(V.tensor_scalar(T.t2[32 * q:32 * q + 32, :], T.tci[0:32, :], 1023, None, op.bitwise_and))
+    for k in range(2):
+        inc(V.tensor_scalar(T.t2[64 * k:64 * k + 64, :], T.tci[0:64, :], 1023, None, op.bitwise_and))
     vw("v", "gi", "fill")
     inc(V.tensor_tensor(T.t3[:, ST * LV:ST * LV + 16], T.t2[:, 0:LC].indirect(T.ooff[:, 0:1]), T.ko[:], op.min))
     inc(V.tensor_tensor(T.t3[:, 0:ST * LV:ST], T.t2[:, 0:LV], T.kl[:, 0:LV], op.min))
@@ -180,28 +187,32 @@ def rank_program(g, core, T, topo):
             wait("a", A, "fg", "tof")
             inc(A.activation(T.vv[:], T.fb[:, 0:FW].indirect(T.toff[:, 0:LV]), COPY), "vg")
     vw("fg")
-    inc(V.transpose(T.tt[:, 0:C], T.fb[:, W0:W0 + C]))
+    inc(V.transpose(T.tt[:, 0:C], T.fb[:, W0:W0 + C]), "tf")
     vw("vg")
     inc(V.transpose(T.tt[:, C:C + NV], T.vv[:]))
+    vw("tf")
+    inc(V.tensor_tensor(T.ta[:], T.tt[:, 0:C:32], T.kf[:], op.min))
+    inc(V.tensor_scalar(T.u0[:], T.tt[:, 0:C:16], float(C), None, op.is_lt))
     vw()
-    inc(V.tensor_tensor(T.ma[:, 0:NB], T.tt[:, 0:C + NV:32], T.tt[:, 16:C + NV:32], op.min))
+    inc(V.tensor_tensor(T.ma[:, 0:BF_], T.ta[:], T.tt[:, 16:C:32], op.min))
+    inc(V.tensor_tensor(T.ma[:, BF_:NB], T.tt[:, C:C + NV:32], T.tt[:, C + 16:C + NV:32], op.min))
+    inc(V.tensor_tensor(T.u1[:], T.u0[:, 0:32:2], T.u0[:, 1:32:2], op.add), "cnt")
     vw()
     inc(V.tensor_tensor(T.mb[0:64, 0:NB], T.ma[0:64, 0:NB], T.ma[64:128, 0:NB], op.min))
     vw()
     inc(V.tensor_tensor(T.r[0:32, 0:NB], T.mb[0:32, 0:NB], T.mb[32:64, 0:NB], op.min))
-    vw()
-    inc(V.tensor_tensor(T.r[0:32, 0:BF_], T.r[0:32, 0:BF_], T.kf[0:32, :], op.min))
-    vw()
-    inc(V.transpose(T.z[0:32, 16:48], T.r[0:32, 0:32]))
-    vw()
-    inc(V.tensor_copy(T.z[0:32, 0:16], T.z[0:32, 16:32]))
-    inc(V.tensor_copy(T.z[0:32, 48:64], T.z[0:32, 32:48]))
+    vw("v", "cnt")
+    for k in range(2):
+        inc(V.transpose(T.z[0:32, k:4:2, :], T.r[0:32, 0:32]))
+    inc(V.tensor_tensor(T.u2[0:64, :], T.u1[0:64, :], T.u1[64:128, :], op.add))
     vw()
     for k in range(2):
-        inc(V.transpose(T.y[0:32, k:64:2], T.z[0:32, 32 * k:32 * k + 32]))
+        inc(V.transpose(T.y[0:32, k:64:2], T.z[0:32, 2 * k:2 * k + 2, :]))
+    inc(V.tensor_tensor(T.r[0:32, 32:32 + BF_], T.u2[0:32, :], T.u2[32:64, :], op.add))
     vw()
     for q in range(4):
         inc(V.tensor_scalar(T.lst[32 * q:32 * q + 32, 0:2 * NB], T.y[0:32, 0:2 * NB], float(MID), None, op.add), "listr")
+    inc(V.transpose(T.ut[0:32, :], T.r[0:32, 32:64]), "utr")
 
     def product(ps, b, n, e, es, x, xs, at, start, stop):
         return P.matmul_mx(ps[:, 512 * b:512 * b + n], e[:, 128 * b:128 * b + 128], es[:, 128 * b:128 * b + 128],
@@ -212,12 +223,13 @@ def rank_program(g, core, T, topo):
         wait("p", P, "wc" + name, "wp" + name)
         for b in range(4):
             product(ps, b, n, T.q1, T.q1s, T.wsl, T.wsls, at, True, False)
-    wait("p", P, "eq2", "arc", "ownc", "ars", "owns")
-    for name, ps, at, n, m in halves:
+    for hf, arrived in ((1 - mine, ("eq2", "arc0", "ars0")), (mine, ("arc1", "ars1", "ownc", "owns"))):
+        name, ps, at, n, m = halves[hf]
+        wait("p", P, *arrived)
         for b in range(4):
             product(ps, b, n, T.q2, T.q2s, T.land, T.lands, at, False, False)
-    vw("listr", "arc", "ownc")
-    wait("a", A, "listr", "ars", "owns")
+    vw("listr", "arc0", "arc1", "ownc")
+    wait("a", A, "listr", "ars0", "ars1", "owns")
     for name, ps, at, n, m in halves:
         off = T.lst[:, 2 * BF_ + at // 16:2 * BF_ + (at + m) // 16]
         inc(V.tensor_copy(u32(T.pk[:, at:at + m]), u32(T.land[:, 0:NS + ZC]).indirect(off)), "pc" + name)
@@ -225,15 +237,6 @@ def rank_program(g, core, T, topo):
         wait("p", P, "pc" + name, "pp" + name)
         for b in range(4):
             inc(product(ps, b, m, T.q2, T.q2s, T.pk, T.pks, at, False, True), "t%s%d" % (name, b))
-    inc(V.tensor_scalar(T.u0[:], T.tt[:, 0:C:16], float(C), None, op.is_lt))
-    vw()
-    inc(V.tensor_tensor(T.u1[:], T.u0[:, 0:32:2], T.u0[:, 1:32:2], op.add))
-    vw()
-    inc(V.tensor_tensor(T.u2[0:64, :], T.u1[0:64, :], T.u1[64:128, :], op.add))
-    vw()
-    inc(V.tensor_tensor(T.r[0:32, 32:32 + BF_], T.u2[0:32, :], T.u2[32:64, :], op.add))
-    vw()
-    inc(V.transpose(T.ut[0:32, :], T.r[0:32, 32:64]), "utr")
 
     for name, ps, at, n, m in halves:
         for b in range(4):
@@ -245,19 +248,19 @@ def rank_program(g, core, T, topo):
                 wait("a", A, "t%s%d" % (name, b))
                 inc(A.activation(out, src, COPY), "hs" + name)
         vw("v", "hs" + name)
-        inc(V.quantize_mx(T.wn[:, at:at + n], T.wns[:, at:at + n], T.h[:, 4 * at:4 * (at + n)]), "qn" + name)
+        inc(V.quantize_mx(T.wn[:, at:at + n], T.wns[:, at:at + n], T.h[:, 4 * at:4 * (at + n)]), "qn")
 
-    vw("ldn", "qna", "qnb")
-    wait("a", A, "ldn", "qna", "qnb")
-    for k in range(2):
-        off = T.lst[:, 16 * k:16 * k + 16]
-        inc(V.tensor_copy(u32(T.on[:, 256 * k:256 * k + 256]), u32(T.wn[:, 0:NS + C]).indirect(off)), "onc%d" % k)
-    inc(A.activation(T.ons[:], T.wns[:, 0:NS + C].indirect(T.lst[:, 0:32]), COPY), "ons0")
     wait("y", Y, "utr")
     inc(Y.dma_start(T.up[:], T.ut[0:16, :]), "st", 16)
-    for k in range(2):
+    vw("ldn", "qn")
+    wait("a", A, "ldn", "qn")
+    inc(A.activation(T.ons[:], T.wns[:, 0:NS + C].indirect(T.lst[:, 0:32]), COPY), "ons0")
+    a = 0
+    for k, n in enumerate(CHUNKS):
+        inc(V.tensor_copy(u32(T.on[:, 16 * a:16 * (a + n)]), u32(T.wn[:, 0:NS + C]).indirect(T.lst[:, a:a + n])), "onc%d" % k)
         wait("y", Y, "onc%d" % k)
-        inc(Y.dma_start(T.oc[:, 1024 * k:1024 * k + 1024], u8(T.on[:, 256 * k:256 * k + 256])), "st", 16)
+        inc(Y.dma_start(T.oc[:, 64 * a:64 * (a + n)], u8(T.on[:, 16 * a:16 * (a + n)])), "st", 16)
+        a += n
     for k in range(4):
         qn, q = (("a", A), ("y", Y))[k // 3]
         wait(qn, q, "ons0")

@@ -31,7 +31,7 @@ SCRATCH = {
     "pk": ("sbuf", [128, NS], X4), "pks": ("sbuf", [128, NS], U8),
     "wn": ("sbuf", [128, NS + C], X4), "wns": ("sbuf", [128, NS + C], U8),
     "on": ("sbuf", [128, C], X4), "ons": ("sbuf", [128, C], U8),
-    "eb": ("sbuf", [128, EW], "bfloat16"), "e2": ("sbuf", [128, EW], "bfloat16"),
+    "ee": ("sbuf", [128, 2 * EW], "bfloat16"), "jp": ("sbuf", [128, 128], "bfloat16"),
     "q1": ("sbuf", [128, 512 + ZC], X4), "q1s": ("sbuf", [128, 512 + ZC], U8),
     "q2": ("sbuf", [128, 512], X4), "q2s": ("sbuf", [128, 512], U8),
     "pn": ("sbuf", [128, 2], "int32"), "ooff": ("sbuf", [128, 2], "uint16"),
@@ -51,7 +51,7 @@ SCRATCH = {
     "h": ("sbuf", [128, 4 * NS], "bfloat16"),
     "psa": ("psum", [128, 2048], "float32"), "psb": ("psum", [128, 2048], "float32"),
 }
-SEMAPHORES = ["ldg0", "ldg1", "gpc0", "gpc1", "gpp0", "gpp1", "arc0", "arc1", "ars0", "ars1", "tf", "cnt", "hsa", "hsb", "lds", "ldt", "ldw", "ldn", "ownc", "owns", "st", "sent", "v", "z1", "z2", "fill", "gp0", "gi", "ea", "e2r",
+SEMAPHORES = ["fbn", "gpc2", "ldg0", "ldg1", "gpc0", "gpc1", "gpp0", "gpp1", "arc0", "arc1", "ars0", "ars1", "tf", "cnt", "hsa", "hsb", "lds", "ldt", "ldw", "ldn", "ownc", "owns", "st", "sent", "v", "z1", "fill", "gp0", "gi", "ea",
               "eq1", "eq2", "soffr", "gqr", "woffr", "tof", "fg", "vg", "listr", "utr", "qn", "ons0"] + \
              ["onc%d" % k for k in range(len(CHUNKS))] + \
              [k + h for k in ("wc", "wp", "pc", "pp") for h in "ab"] + ["t%s%d" % (h, b) for h in "ab" for b in range(4)]
@@ -97,32 +97,34 @@ def rank_program(g, core, T, topo):
     inc(A.dma_start(T.w2s[:], T.ws[:]), "ldw", 16)
 
     F32 = {"allow_small_or_imprecise_dtypes": True}
-    inc(V.memset(T.eb[:], 0.0), "z1")
-    inc(V.memset(T.e2[:], 0.0), "z2")
+    inc(V.memset(T.ee[:], 0.0), "z1")
+    inc(g.iota(T.jp[:], [[1, 128]], 0, -1, **F32), "z1")
     inc(g.iota(T.pn[:], [[0, 2]], 0, 1), "gp0")
-    for e, zz, fill, name in ((T.eb, "z1", 1.0, "ea"), (T.e2, "z2", -0.125, "e2r")):
-        wait("g", g, zz)
-        inc(g.affine_select(e[:, 3:515:4], e[:, 3:515:4], [[1, 128]], op.not_equal, fill, 0, -1), name)
+    vw("z1")
+    for at, fill in ((0, 1.0), (EW, -0.125)):
+        inc(V.tensor_scalar(T.ee[:, at + 3:at + 515:4], T.jp[:], 0.0, fill, op.is_equal, op.mult), "ea")
     inc(g.iota(T.kl[:], [[-9600, N], [0, 3]], -9040, 600), "gi")
     inc(g.iota(T.ko[:], [[3, 16]], C, 1), "gi")
     inc(g.iota(T.vals[:], [[1, CAPP]], -MID, 3, **F32), "gi")
     inc(g.iota(T.kf[:], [[32, BF_]], NS - MID, 1, **F32), "gi")
-    inc(V.memset(T.fb[:, 0:W0], float(NS - MID)), "fill")
-    inc(V.memset(T.fb[:, W0:FW], float(NONE)), "fill")
-    inc(V.memset(T.r[:], 0.0), "fill")
+    wait("a", A, "ea")
+    for out, n, fill in ((T.fb[:, W0:FW], FW - W0, NONE), (T.fb[:, 0:W0], W0, NS - MID), (T.r[:], 64, 0)):
+        inc(A.activation(out, T.ee[:, 0:n], ActivationFunctionType.Identity, bias=float(fill), scale=0.0), "fbn")
     vw("gp0")
     inc(V.tensor_scalar(T.ooff[:], T.pn[:], 3 / 16, float(LC - 1), op.mult, op.min), "fill")
     vw("ea")
     for b in range(4):
         n = 128 + ZC * (b == 3)
-        inc(V.quantize_mx(T.q1[:, 128 * b:128 * b + n], T.q1s[:, 128 * b:128 * b + n], T.eb[:, 3 - b:3 - b + 4 * n]), "eq1")
+        inc(V.quantize_mx(T.q1[:, 128 * b:128 * b + n], T.q1s[:, 128 * b:128 * b + n], T.ee[:, 3 - b:3 - b + 4 * n]), "eq1")
     wait("y", Y, "eq1")
     inc(Y.dma_start(u8(T.land[:, NS:NS + ZC]), u8(T.q1[:, 512:512 + ZC])), "ownc", 16)
     inc(Y.dma_start(T.lands[:, NS:NS + ZC], T.q1s[:, 512:512 + ZC]), "owns", 16)
 
-    vw("e2r")
-    for b in range(4):
-        inc(V.quantize_mx(T.q2[:, 128 * b:128 * b + 128], T.q2s[:, 128 * b:128 * b + 128], T.e2[:, 3 - b:515 - b]), "eq2")
+    def second(b):
+        inc(V.quantize_mx(T.q2[:, 128 * b:128 * b + 128], T.q2s[:, 128 * b:128 * b + 128], T.ee[:, EW + 3 - b:EW + 515 - b]), "eq2")
+
+    second(0)
+    second(1)
 
     lo = CAPP * rank
     vw("lds")
@@ -135,27 +137,44 @@ def rank_program(g, core, T, topo):
     wait("a", A, "soffr", "gqr")
     H = N // 2
     mine = rank // H
-    total["sent"] = 0
-    for wave, hf in enumerate((1 - mine, mine)):
-        off = T.soff[:, LC // 2 * hf:LC // 2 * (hf + 1)]
-        inc(V.tensor_copy(u32(T.gp[:, HALF * hf:HALF * (hf + 1)]), u32(T.gq[:, 0:S]).indirect(off)), "gpc%d" % wave)
-        inc(A.activation(T.gps[:, HALF * hf:HALF * (hf + 1)], T.gqs[:, 0:S].indirect(off), COPY), "gpp%d" % wave)
-        dests = [H * hf + (rank + k) % H for k in range(wave, H)]
-        shares = ([(0, 1), (2, 3), (4, 5), (6, 7)], [(0, 2, 4, 6), (1, 3), (5, 7)])[wave]
-        for scales in (False, True):
-            out, sem = [], ("ars%d" if scales else "arc%d") % wave
-            for q, share in zip(dests, shares):
-                d = T.cores[q]
-                rid, pid = topo.addr(d, core)
-                a = CAPP * q
-                src = T.gps[:, a:a + CAPP] if scales else u8(T.gp[:, a:a + CAPP])
-                dst = T.lands[:, lo:lo + CAPP] if scales else u8(T.land[:, lo:lo + CAPP])
-                out.append(RemoteDMATransfer(dst_ids=[DstId(rid=rid, pnc=pid)], dma_engine_mask=sum(1 << topo.engines(core, d)[e] for e in share),
-                                             remote_sem=T.sem[sem], src=src, dst=dst))
-            wait("g", g, ("gpp%d" if scales else "gpc%d") % wave)
-            g.remote_dma_fused(out, local_sem=T.sem.sent)
-            total[sem] = sum(len(share) for share in shares)
-            total["sent"] += total[sem]
+    for name in ("sent", "arc0", "arc1", "ars0", "ars1"):
+        total[name] = 0
+
+    def pick(a, b, codes, scales):
+        off = T.soff[:, 3 * a:3 * b]
+        inc(V.tensor_copy(u32(T.gp[:, CAPP * a:CAPP * b]), u32(T.gq[:, 0:S]).indirect(off)), codes)
+        inc(A.activation(T.gps[:, CAPP * a:CAPP * b], T.gqs[:, 0:S].indirect(off), COPY), scales)
+
+    def send(dests, shares, scales, ready, sem):
+        out = []
+        for q, share in zip(dests, shares):
+            d = T.cores[q]
+            rid, pid = topo.addr(d, core)
+            a = CAPP * q
+            src = T.gps[:, a:a + CAPP] if scales else u8(T.gp[:, a:a + CAPP])
+            dst = T.lands[:, lo:lo + CAPP] if scales else u8(T.land[:, lo:lo + CAPP])
+            out.append(RemoteDMATransfer(dst_ids=[DstId(rid=rid, pnc=pid)], dma_engine_mask=sum(1 << topo.engines(core, d)[e] for e in share),
+                                         remote_sem=T.sem[sem], src=src, dst=dst))
+            total[sem] += len(share)
+            total["sent"] += len(share)
+        wait("g", g, ready)
+        g.remote_dma_fused(out, local_sem=T.sem.sent)
+
+    E = range(8)
+    for k in range(2):
+        a = H * (1 - mine) + 2 * ((rank // 2 + k) % 2)
+        pick(a, a + 2, "gpc%d" % (2 * k), "gpp0")
+        send([a + rank % 2, a + 1 - rank % 2], [E[0::2], E[1::2]], False, "gpc%d" % (2 * k), "arc0")
+    send([H * (1 - mine) + (rank + k) % H for k in range(H)], [E[2 * k:2 * k + 2] for k in range(H)], True, "gpp0", "ars0")
+    vw("ldt")
+    for k in range(2):
+        inc(V.tensor_scalar(T.t2[64 * k:64 * k + 64, :], T.tci[0:64, :], 1023, None, op.bitwise_and))
+    pick(H * mine, H * mine + H, "gpc1", "gpp1")
+    near = [H * mine + (rank + k) % H for k in range(1, H)]
+    send(near[0:2], [E[0::2], E[1::2]], False, "gpc1", "arc1")
+    send(near[2:3], [E], False, "gpc1", "arc1")
+    send(near[0:2], [E[0::2], E[1::2]], True, "gpp1", "ars1")
+    send(near[2:3], [E], True, "gpp1", "ars1")
     wait("y", Y, "gpc1")
     inc(Y.dma_start(u8(T.land[:, lo:lo + CAPP]), u8(T.gp[:, lo:lo + CAPP])), "ownc", 16)
     wait("y", Y, "gpp1")
@@ -164,15 +183,14 @@ def rank_program(g, core, T, topo):
     inc(Y.dma_start(u8(T.wn[:, NS:NS + C]), T.wc[:]), "ldn", 16)
     inc(Y.dma_start(T.wns[:, NS:NS + C], T.ws[:]), "ldn", 16)
 
-    vw("ldt")
-    for k in range(2):
-        inc(V.tensor_scalar(T.t2[64 * k:64 * k + 64, :], T.tci[0:64, :], 1023, None, op.bitwise_and))
-    vw("v", "gi", "fill")
+    vw("v", "gi", "fill", "fbn")
     inc(V.tensor_tensor(T.t3[:, ST * LV:ST * LV + 16], T.t2[:, 0:LC].indirect(T.ooff[:, 0:1]), T.ko[:], op.min))
     inc(V.tensor_tensor(T.t3[:, 0:ST * LV:ST], T.t2[:, 0:LV], T.kl[:, 0:LV], op.min))
     inc(V.tensor_scalar(T.woff[:], T.t2[:], float(C - 1), None, op.min), "woffr")
+    second(2)
     vw()
     inc(V.tensor_scalar(T.toff[:, 0:LV + 3], T.t3[:, 0:ST * (LV + 2) + 1:ST], float(W0), float(FW - 1), op.add, op.min), "tof")
+    second(3)
     vw("tof")
     inc(V.tensor_copy(T.fb[:, 0:FW].indirect(T.toff[:, LV:LV + 3]), T.vals[:]), "fg")
 
@@ -230,6 +248,7 @@ def rank_program(g, core, T, topo):
             product(ps, b, n, T.q2, T.q2s, T.land, T.lands, at, False, False)
     vw("listr", "arc0", "arc1", "ownc")
     wait("a", A, "listr", "ars0", "ars1", "owns")
+    halves = halves[::-1]
     for name, ps, at, n, m in halves:
         off = T.lst[:, 2 * BF_ + at // 16:2 * BF_ + (at + m) // 16]
         inc(V.tensor_copy(u32(T.pk[:, at:at + m]), u32(T.land[:, 0:NS + ZC]).indirect(off)), "pc" + name)

from concourse.bass import DstId, RemoteDMATransfer
from concourse.mybir import dt, AluOpType as op, ActivationFunctionType

CHUNKS = (18, 14)
X4, U8 = "float8_e4m3fn_x4", "uint8"
C, S, CAPP, N = 512, 256, 48, 8
NS = N * CAPP
HALF = NS // 2
ZC = 2
NP = NS - CAPP
NV = 352
W0 = 16
FW = W0 + C + 176
MID, NONE = 192, 768
LC = NS // 16
LV = NV // 16
ST = 6
BF_, BV = C // 32, NV // 32
NB = BF_ + BV
EW = 520

SCRATCH = {
    "grt": ("sbuf", [128, 4 * S], "bfloat16"),
    "sni": ("sbuf", [128, LC], "int32"), "tci": ("sbuf", [128, LC], "int32"),
    "soff": ("sbuf", [128, LC], "uint16"), "woff": ("sbuf", [128, LC], "uint16"),
    "gq": ("sbuf", [128, S], X4), "gqs": ("sbuf", [128, S], U8),
    "gp": ("sbuf", [128, NS], X4), "gps": ("sbuf", [128, NS], U8),
    "land": ("sbuf", [128, NS + ZC], X4), "lands": ("sbuf", [128, NS + ZC], U8),
    "w2": ("sbuf", [128, C], X4), "w2s": ("sbuf", [128, C], U8),
    "wsl": ("sbuf", [128, NS], X4), "wsls": ("sbuf", [128, NS], U8),
    "pk": ("sbuf", [128, NS], X4), "pks": ("sbuf", [128, NS], U8),
    "wn": ("sbuf", [128, NS + C], X4), "wns": ("sbuf", [128, NS + C], U8),
    "on": ("sbuf", [128, C], X4), "ons": ("sbuf", [128, C], U8),
    "ee": ("sbuf", [128, 2 * EW], "bfloat16"), "jp": ("sbuf", [128, 128], "bfloat16"),
    "q1": ("sbuf", [128, 512 + ZC], X4), "q1s": ("sbuf", [128, 512 + ZC], U8),
    "q2": ("sbuf", [128, 512], X4), "q2s": ("sbuf", [128, 512], U8),
    "pn": ("sbuf", [128, 2], "int32"), "ooff": ("sbuf", [128, 2], "uint16"),
    "kl": ("sbuf", [128, LC], "int32"), "ko": ("sbuf", [128, 16], "int32"),
    "t2": ("sbuf", [128, LC], "int32"), "t3": ("sbuf", [128, ST * LV + 16], "int32"),
    "toff": ("sbuf", [128, LV + 4], "uint16"),
    "vals": ("sbuf", [128, CAPP], "bfloat16"),
    "fb": ("sbuf", [128, FW], "bfloat16"),
    "vv": ("sbuf", [128, NV], "bfloat16"),
    "tt": ("sbuf", [128, C + NV], "bfloat16"),
    "ma": ("sbuf", [128, 32], "float32"), "mb": ("sbuf", [128, 32], "float32"),
    "kf": ("sbuf", [128, 16], "float32"), "ta": ("sbuf", [128, 16], "float32"),
    "r": ("sbuf", [128, 64], "float32"), "z": ("sbuf", [128, 4, 16], "float32"), "y": ("sbuf", [128, 64], "float32"),
    "lst": ("sbuf", [128, 64], "uint16"),
    "u0": ("sbuf", [128, 32], "float32"), "u1": ("sbuf", [128, 16], "float32"), "u2": ("sbuf", [128, 16], "float32"),
    "ut": ("sbuf", [128, 32], "float32"),
    "h": ("sbuf", [128, 4 * NS], "bfloat16"),
    "psa": ("psum", [128, 2048], "float32"), "psb": ("psum", [128, 2048], "float32"),
}
SEMAPHORES = ["fbn", "gpc2", "ldg0", "ldg1", "gpc0", "gpc1", "gpp0", "gpp1", "arc0", "arc1", "ars0", "ars1", "tf", "cnt", "hsa", "hsb", "lds", "ldt", "ldw", "ldn", "ownc", "owns", "st", "sent", "v", "z1", "fill", "gp0", "gi", "ea",
              "eq1", "eq2", "soffr", "gqr", "woffr", "tof", "fg", "vg", "listr", "utr", "qn", "ons0"] + \
             ["onc%d" % k for k in range(len(CHUNKS))] + \
             [k + h for k in ("wc", "wp", "pc", "pp") for h in "ab"] + ["t%s%d" % (h, b) for h in "ab" for b in range(4)]


def u8(v):
    return v.bitcast(dt.uint8)


def u32(v):
    return v.bitcast(dt.uint32)


def rank_program(g, core, T, topo):
    rank = T.rank_of(core)
    if rank is None:
        return
    V, P, A, Y = g.vector, g.tensor, g.scalar, g.sync
    COPY = ActivationFunctionType.Copy
    total, seen = {}, {}

    def inc(ins, name="v", n=1):
        ins.then_inc(T.sem[name], n)
        total[name] = total.get(name, 0) + n
        return name

    def wait(qn, q, *evs):
        for name in evs:
            if seen.get((qn, name), 0) < total[name]:
                q.wait_ge(T.sem[name], total[name])
                seen[(qn, name)] = total[name]

    def vw(*evs):
        wait("v", V, *(evs or ("v",)))

    for k in range(2):
        inc(Y.dma_start(T.grt[:, 2 * S * k:2 * S * (k + 1)], T.gr[:, 2 * S * k:2 * S * (k + 1)]), "ldg%d" % k, 16)
    for k in range(4):
        inc(A.dma_start(T.sni[16 * k:16 * k + 16, :], T.sn[:]), "lds", 16)
    for k, q in enumerate((Y, Y, Y, A)):
        inc(q.dma_start(T.tci[16 * k:16 * k + 16, :], T.tc[:]), "ldt", 16)
    inc(Y.dma_start(u8(T.w2[:]), T.wc[:]), "ldw", 16)
    inc(A.dma_start(T.w2s[:], T.ws[:]), "ldw", 16)

    F32 = {"allow_small_or_imprecise_dtypes": True}
    inc(V.memset(T.ee[:], 0.0), "z1")
    inc(g.iota(T.jp[:], [[1, 128]], 0, -1, **F32), "z1")
    inc(g.iota(T.pn[:], [[0, 2]], 0, 1), "gp0")
    vw("z1")
    for at, fill in ((0, 1.0), (EW, -0.125)):
        inc(V.tensor_scalar(T.ee[:, at + 3:at + 515:4], T.jp[:], 0.0, fill, op.is_equal, op.mult), "ea")
    inc(g.iota(T.kl[:], [[-9600, N], [0, 3]], -9040, 600), "gi")
    inc(g.iota(T.ko[:], [[3, 16]], C, 1), "gi")
    inc(g.iota(T.vals[:], [[1, CAPP]], -MID, 3, **F32), "gi")
    inc(g.iota(T.kf[:], [[32, BF_]], NS - MID, 1, **F32), "gi")
    wait("a", A, "ea")
    for out, n, fill in ((T.fb[:, W0:FW], FW - W0, NONE), (T.fb[:, 0:W0], W0, NS - MID), (T.r[:], 64, 0)):
        inc(A.activation(out, T.ee[:, 0:n], ActivationFunctionType.Identity, bias=float(fill), scale=0.0), "fbn")
    vw("gp0")
    inc(V.tensor_scalar(T.ooff[:], T.pn[:], 3 / 16, float(LC - 1), op.mult, op.min), "fill")
    vw("ea")
    for b in range(4):
        n = 128 + ZC * (b == 3)
        inc(V.quantize_mx(T.q1[:, 128 * b:128 * b + n], T.q1s[:, 128 * b:128 * b + n], T.ee[:, 3 - b:3 - b + 4 * n]), "eq1")
    wait("y", Y, "eq1")
    inc(Y.dma_start(u8(T.land[:, NS:NS + ZC]), u8(T.q1[:, 512:512 + ZC])), "ownc", 16)
    inc(Y.dma_start(T.lands[:, NS:NS + ZC], T.q1s[:, 512:512 + ZC]), "owns", 16)

    def second(b):
        inc(V.quantize_mx(T.q2[:, 128 * b:128 * b + 128], T.q2s[:, 128 * b:128 * b + 128], T.ee[:, EW + 3 - b:EW + 515 - b]), "eq2")

    second(0)
    second(1)

    lo = CAPP * rank
    vw("lds")
    for k in range(2):
        inc(V.tensor_copy(T.soff[64 * k:64 * k + 64, :], T.sni[0:64, :]), "soffr")
    for k in range(2):
        vw("ldg%d" % k)
        inc(V.quantize_mx(T.gq[:, 128 * k:128 * k + 128], T.gqs[:, 128 * k:128 * k + 128], T.grt[:, 2 * S * k:2 * S * (k + 1)]), "gqr")
    vw("gqr", "soffr")
    wait("a", A, "soffr", "gqr")
    H = N // 2
    mine = rank // H
    for name in ("sent", "arc0", "arc1", "ars0", "ars1"):
        total[name] = 0

    def pick(a, b, codes, scales):
        off = T.soff[:, 3 * a:3 * b]
        inc(V.tensor_copy(u32(T.gp[:, CAPP * a:CAPP * b]), u32(T.gq[:, 0:S]).indirect(off)), codes)
        inc(A.activation(T.gps[:, CAPP * a:CAPP * b], T.gqs[:, 0:S].indirect(off), COPY), scales)

    def send(dests, shares, scales, ready, sem):
        out = []
        for q, share in zip(dests, shares):
            d = T.cores[q]
            rid, pid = topo.addr(d, core)
            a = CAPP * q
            src = T.gps[:, a:a + CAPP] if scales else u8(T.gp[:, a:a + CAPP])
            dst = T.lands[:, lo:lo + CAPP] if scales else u8(T.land[:, lo:lo + CAPP])
            out.append(RemoteDMATransfer(dst_ids=[DstId(rid=rid, pnc=pid)], dma_engine_mask=sum(1 << topo.engines(core, d)[e] for e in share),
                                         remote_sem=T.sem[sem], src=src, dst=dst))
            total[sem] += len(share)
            total["sent"] += len(share)
        wait("g", g, ready)
        g.remote_dma_fused(out, local_sem=T.sem.sent)

    E = range(8)
    for k in range(2):
        a = H * (1 - mine) + 2 * ((rank // 2 + k) % 2)
        pick(a, a + 2, "gpc%d" % (2 * k), "gpp0")
        send([a + rank % 2, a + 1 - rank % 2], [E[0::2], E[1::2]], False, "gpc%d" % (2 * k), "arc0")
    send([H * (1 - mine) + (rank + k) % H for k in range(H)], [E[2 * k:2 * k + 2] for k in range(H)], True, "gpp0", "ars0")
    vw("ldt")
    for k in range(2):
        inc(V.tensor_scalar(T.t2[64 * k:64 * k + 64, :], T.tci[0:64, :], 1023, None, op.bitwise_and))
    pick(H * mine, H * mine + H, "gpc1", "gpp1")
    near = [H * mine + (rank + k) % H for k in range(1, H)]
    send(near[0:2], [E[0::2], E[1::2]], False, "gpc1", "arc1")
    send(near[2:3], [E], False, "gpc1", "arc1")
    send(near[0:2], [E[0::2], E[1::2]], True, "gpp1", "ars1")
    send(near[2:3], [E], True, "gpp1", "ars1")
    wait("y", Y, "gpc1")
    inc(Y.dma_start(u8(T.land[:, lo:lo + CAPP]), u8(T.gp[:, lo:lo + CAPP])), "ownc", 16)
    wait("y", Y, "gpp1")
    inc(Y.dma_start(T.lands[:, lo:lo + CAPP], T.gps[:, lo:lo + CAPP]), "owns", 16)
    wait("y", Y, "sent")
    inc(Y.dma_start(u8(T.wn[:, NS:NS + C]), T.wc[:]), "ldn", 16)
    inc(Y.dma_start(T.wns[:, NS:NS + C], T.ws[:]), "ldn", 16)

    vw("v", "gi", "fill", "fbn")
    inc(V.tensor_tensor(T.t3[:, ST * LV:ST * LV + 16], T.t2[:, 0:LC].indirect(T.ooff[:, 0:1]), T.ko[:], op.min))
    inc(V.tensor_tensor(T.t3[:, 0:ST * LV:ST], T.t2[:, 0:LV], T.kl[:, 0:LV], op.min))
    inc(V.tensor_scalar(T.woff[:], T.t2[:], float(C - 1), None, op.min), "woffr")
    second(2)
    vw()
    inc(V.tensor_scalar(T.toff[:, 0:LV + 3], T.t3[:, 0:ST * (LV + 2) + 1:ST], float(W0), float(FW - 1), op.add, op.min), "tof")
    second(3)
    vw("tof")
    inc(V.tensor_copy(T.fb[:, 0:FW].indirect(T.toff[:, LV:LV + 3]), T.vals[:]), "fg")

    halves = (("a", T.psa, 0, HALF, HALF), ("b", T.psb, HALF, HALF, NP - HALF))
    vw("woffr", "ldw")
    wait("a", A, "woffr", "ldw")
    for name, ps, at, n, m in halves:
        off = T.woff[:, at // 16:(at + n) // 16]
        inc(V.tensor_copy(u32(T.wsl[:, at:at + n]), u32(T.w2[:, 0:C]).indirect(off)), "wc" + name)
        inc(A.activation(T.wsls[:, at:at + n], T.w2s[:, 0:C].indirect(off), COPY), "wp" + name)
        if name == "a":
            wait("a", A, "fg", "tof")
            inc(A.activation(T.vv[:], T.fb[:, 0:FW].indirect(T.toff[:, 0:LV]), COPY), "vg")
    vw("fg")
    inc(V.transpose(T.tt[:, 0:C], T.fb[:, W0:W0 + C]), "tf")
    vw("vg")
    inc(V.transpose(T.tt[:, C:C + NV], T.vv[:]))
    vw("tf")
    inc(V.tensor_tensor(T.ta[:], T.tt[:, 0:C:32], T.kf[:], op.min))
    inc(V.tensor_scalar(T.u0[:], T.tt[:, 0:C:16], float(C), None, op.is_lt))
    vw()
    inc(V.tensor_tensor(T.ma[:, 0:BF_], T.ta[:], T.tt[:, 16:C:32], op.min))
    inc(V.tensor_tensor(T.ma[:, BF_:NB], T.tt[:, C:C + NV:32], T.tt[:, C + 16:C + NV:32], op.min))
    inc(V.tensor_tensor(T.u1[:], T.u0[:, 0:32:2], T.u0[:, 1:32:2], op.add), "cnt")
    vw()
    inc(V.tensor_tensor(T.mb[0:64, 0:NB], T.ma[0:64, 0:NB], T.ma[64:128, 0:NB], op.min))
    vw()
    inc(V.tensor_tensor(T.r[0:32, 0:NB], T.mb[0:32, 0:NB], T.mb[32:64, 0:NB], op.min))
    vw("v", "cnt")
    for k in range(2):
        inc(V.transpose(T.z[0:32, k:4:2, :], T.r[0:32, 0:32]))
    inc(V.tensor_tensor(T.u2[0:64, :], T.u1[0:64, :], T.u1[64:128, :], op.add))
    vw()
    for k in range(2):
        inc(V.transpose(T.y[0:32, k:64:2], T.z[0:32, 2 * k:2 * k + 2, :]))
    inc(V.tensor_tensor(T.r[0:32, 32:32 + BF_], T.u2[0:32, :], T.u2[32:64, :], op.add))
    vw()
    for q in range(4):
        inc(V.tensor_scalar(T.lst[32 * q:32 * q + 32, 0:2 * NB], T.y[0:32, 0:2 * NB], float(MID), None, op.add), "listr")
    inc(V.transpose(T.ut[0:32, :], T.r[0:32, 32:64]), "utr")

    def product(ps, b, n, e, es, x, xs, at, start, stop):
        return P.matmul_mx(ps[:, 512 * b:512 * b + n], e[:, 128 * b:128 * b + 128], es[:, 128 * b:128 * b + 128],
                           x[:, at:at + n], xs[:, at:at + n], start, stop)

    wait("p", P, "eq1")
    for name, ps, at, n, m in halves:
        wait("p", P, "wc" + name, "wp" + name)
        for b in range(4):
            product(ps, b, n, T.q1, T.q1s, T.wsl, T.wsls, at, True, False)
    for hf, arrived in ((1 - mine, ("eq2", "arc0", "ars0")), (mine, ("arc1", "ars1", "ownc", "owns"))):
        name, ps, at, n, m = halves[hf]
        wait("p", P, *arrived)
        for b in range(4):
            product(ps, b, n, T.q2, T.q2s, T.land, T.lands, at, False, False)
    vw("listr", "arc0", "arc1", "ownc")
    wait("a", A, "listr", "ars0", "ars1", "owns")
    halves = halves[::-1]
    for name, ps, at, n, m in halves:
        off = T.lst[:, 2 * BF_ + at // 16:2 * BF_ + (at + m) // 16]
        inc(V.tensor_copy(u32(T.pk[:, at:at + m]), u32(T.land[:, 0:NS + ZC]).indirect(off)), "pc" + name)
        inc(A.activation(T.pks[:, at:at + m], T.lands[:, 0:NS + ZC].indirect(off), COPY), "pp" + name)
        wait("p", P, "pc" + name, "pp" + name)
        for b in range(4):
            inc(product(ps, b, m, T.q2, T.q2s, T.pk, T.pks, at, False, True), "t%s%d" % (name, b))

    for name, ps, at, n, m in halves:
        for b in range(4):
            out, src = T.h[:, 4 * at + b:4 * (at + n):4], ps[:, 512 * b:512 * b + n]
            if b % 2 == 0:
                vw("t%s%d" % (name, b))
                inc(V.tensor_copy(out, src))
            else:
                wait("a", A, "t%s%d" % (name, b))
                inc(A.activation(out, src, COPY), "hs" + name)
        vw("v", "hs" + name)
        inc(V.quantize_mx(T.wn[:, at:at + n], T.wns[:, at:at + n], T.h[:, 4 * at:4 * (at + n)]), "qn")

    wait("y", Y, "utr")
    inc(Y.dma_start(T.up[:], T.ut[0:16, :]), "st", 16)
    vw("ldn", "qn")
    wait("a", A, "ldn", "qn")
    inc(A.activation(T.ons[:], T.wns[:, 0:NS + C].indirect(T.lst[:, 0:32]), COPY), "ons0")
    a = 0
    for k, n in enumerate(CHUNKS):
        inc(V.tensor_copy(u32(T.on[:, 16 * a:16 * (a + n)]), u32(T.wn[:, 0:NS + C]).indirect(T.lst[:, a:a + n])), "onc%d" % k)
        wait("y", Y, "onc%d" % k)
        inc(Y.dma_start(T.oc[:, 64 * a:64 * (a + n)], u8(T.on[:, 16 * a:16 * (a + n)])), "st", 16)
        a += n
    for k in range(4):
        qn, q = (("a", A), ("y", Y))[k // 3]
        wait(qn, q, "ons0")
        inc(q.dma_start(T.osc[4 * k:4 * k + 4, :], T.ons[32 * k:32 * k + 4, :]), "st", 16)

    for name in total:
        if name not in ("st",):
            wait("g", g, name)
    wait("y", Y, "st")
